import numpy as np
import ml_dtypes


def mxq(x, axis, fmt="e4m3"):
    dtype, down = {"e4m3": (ml_dtypes.float8_e4m3fn, 7), "e5m2": (ml_dtypes.float8_e5m2, 14)}[fmt]
    v = np.moveaxis(np.asarray(x, np.float32).astype(ml_dtypes.bfloat16).astype(np.float64), axis, -1)
    blocks = v.reshape(v.shape[:-1] + (-1, 32))
    amax = np.abs(blocks).max(-1, keepdims=True)
    byte = np.maximum(np.where(amax > 0, np.frexp(amax)[1] - 1 + 127, 0) - down, 1)
    scale = np.exp2(byte - 127.0)
    codes = (blocks / scale).astype(np.float32).astype(dtype).astype(np.float64)
    return np.moveaxis((codes * scale).reshape(v.shape), -1, axis)


WIDE = False


def mx_kscale(k):
    if not WIDE:
        return np.ones(k)
    levels = np.array([10, -10, 5, -5, 0])
    if k % 512:
        return np.exp2(np.random.permutation(np.resize(levels, k // 32))).repeat(32)
    a = np.empty((k // 512, 16))
    for p in range(k // 512):
        a[p, :8] = np.random.permutation(np.resize(levels, 8))
        for g in range(8):
            far = levels[np.abs(levels - a[p, g]) >= 10]
            a[p, g + 8] = far[np.random.randint(len(far))]
    return np.exp2(a.ravel()).repeat(32)


def f64(x):
    return np.asarray(x).astype(np.float64)


def striped(idx):
    return np.tile(idx.reshape(-1, 16).T, (8, 1)).astype(np.uint16)


def unstriped(offs):
    return offs[:16].T.reshape(-1).astype(np.int64)


E2M1 = np.array([0.0, 0.5, 1.0, 1.5, 2.0, 3.0, 4.0, 6.0, -0.0, -0.5, -1.0, -1.5, -2.0, -3.0, -4.0, -6.0])


def pack_weight(w, fmt):
    k, n = w.shape
    w = f64(np.asarray(w, np.float32).astype(ml_dtypes.bfloat16)).reshape(k // 32, 32, n)
    amax = np.abs(w).max(1)
    if fmt == "e4m3":
        byte = np.frexp(amax)[1] - 1 + 127 - 7
    else:
        mant, ex = np.frexp(amax / 6.0)
        byte = np.where(mant > 0.5, ex, ex - 1) + 127
    byte = np.clip(np.where(amax > 0, byte, 1), 1, 254)
    scaled = (w * np.exp2(127.0 - byte)[:, None, :]).reshape(k, n).astype(np.float32)
    by_word = np.ascontiguousarray(scaled.reshape(k // 512, 128, 4, n).transpose(0, 1, 3, 2))
    if fmt == "e4m3":
        words = by_word.astype(ml_dtypes.float8_e4m3fn).view(np.uint8)
    else:
        c = by_word.astype(ml_dtypes.float4_e2m1fn).view(np.uint8) & 0xF
        words = (c[..., 0::2] | (c[..., 1::2] << 4)).reshape(k // 512, 128, 2 * n)
    return np.ascontiguousarray(words), np.ascontiguousarray(byte.astype(np.uint8).reshape(k // 512, 16, n))


def unpack_weight(words, scales, fmt):
    g, _, n = scales.shape
    words = np.ascontiguousarray(words).reshape(g, 128, n, -1)
    if fmt == "e4m3":
        vals = words.view(ml_dtypes.float8_e4m3fn).astype(np.float64)
    else:
        nib = np.empty((g, 128, n, 4), np.uint8)
        nib[..., 0::2] = words & 0xF
        nib[..., 1::2] = words >> 4
        vals = E2M1[nib]
    vals = vals * np.repeat(np.exp2(scales.astype(np.float64) - 127.0), 8, axis=1)[..., None]
    return vals.transpose(0, 1, 3, 2).reshape(g * 512, n)


K, T, E, C, H, N = 1024, 768, 3, 256, 512, 512


def by_expert(wq, xq):
    return np.concatenate([wq[e].T @ xq[:, e * C:(e + 1) * C] for e in range(E)], axis=1)


def setup_inputs():
    n = np.random.standard_normal
    s = mx_kscale(K)
    u = mx_kscale(H)
    slot_token = np.random.permutation(T)[:E * C]
    partner = np.concatenate([np.random.permutation(T) for _ in range(-(-E * C // T))])[:E * C]
    x = pack_weight(n((K, T)) * s[:, None], "e4m3")
    wp = [pack_weight(m, "e2m1") for m in n((E, K, H)) / np.sqrt(K) / s[None, :, None] * u]
    return {
        "x_words": x[0],
        "x_scales": x[1],
        "w1": (n((E, K, H)) / np.sqrt(K) / s[None, :, None] * u).astype(np.float32),
        "wp_words": np.stack([m[0] for m in wp]),
        "wp_scales": np.stack([m[1] for m in wp]),
        "w2": (n((E, H, N)) / np.sqrt(H) / u[None, :, None]).astype(np.float32),
        "gate": np.tile(np.random.uniform(0.2, 1.0, E * C), (128, 1)).astype(np.float32),
        "offs": striped(slot_token),
        "offs2": striped(partner),
    }


def reference(x_words, x_scales, w1, wp_words, wp_scales, w2, gate, offs, offs2):
    w1q = mxq(f64(w1), 1, "e4m3")
    wp = np.stack([unpack_weight(wp_words[e], wp_scales[e], "e2m1") for e in range(E)])
    w2q = mxq(f64(w2), 1, "e4m3")
    idx, idx2 = unstriped(offs), unstriped(offs2)
    x = unpack_weight(x_words, x_scales, "e4m3")
    h = by_expert(w1q, x[:, idx]) + by_expert(wp, x[:, idx2])
    y = by_expert(w2q, mxq(h, 0, "e4m3"))
    out = np.zeros((N, T))
    out[:, idx] = f64(gate[:1]) * y
    return out

@@ -1,0 +1,216 @@
+from contextlib import ExitStack
+
+import concourse.mybir as mybir
+from concourse.masks import make_identity
+
+K, T, E, C, H, N = 1024, 768, 3, 256, 512, 512
+FLOPS = 2 * E * C * (2 * K * H + H * N)
+
+F32 = mybir.dt.float32
+BF16 = mybir.dt.bfloat16
+I32 = mybir.dt.int32
+U32 = mybir.dt.uint32
+U16 = mybir.dt.uint16
+U8 = mybir.dt.uint8
+FP8X4 = mybir.dt.float8_e4m3fn_x4
+FP4X4 = mybir.dt.float4_e2m1fn_x4
+MULT = mybir.AluOpType.mult
+
+P = 128
+PACK = 4
+K_PASS = P * PACK
+PASSES = K // K_PASS
+QUADS = 4
+HALF = 256
+LINE = 4
+
+
+def tile_moe_duo_none_kernel(
+    tc, x_words, x_scales, w1, wp_words, wp_scales, w2, gate, offs, offs2, out
+):
+    nc = tc.nc
+    with ExitStack() as ctx:
+        keep = ctx.enter_context(tc.tile_pool(name="keep", bufs=1))
+        psum = ctx.enter_context(tc.psum_pool(name="psum", bufs=1))
+
+        def held(shape, dtype, name):
+            return keep.tile(shape, dtype, name=name, align_bytes=64)
+
+        own_list = keep.tile([P, T // 16], U16, name="own_list")
+        mate_list = keep.tile([P, T // 16], U16, name="mate_list")
+        x_win = [held([P, T], I32, f"x_win{s}") for s in range(PASSES)]
+        both_win = held([P, T], U8, "both_win")
+        last_win = held([P, T], U8, "last_win")
+        wp_plane = held([P, E * PASSES, H], U8, "wp_plane")
+        wp_sb = [held([P, PASSES, 2 * H], U8, f"wp_sb{e}") for e in range(E)]
+        gate_sb = held([P, T], F32, "gate_sb")
+        ident = held([P, P], F32, "ident")
+
+        nc.vector.memset(both_win[:].bitcast(I32), 0)
+        nc.vector.memset(last_win[:].bitcast(I32), 0)
+        nc.vector.memset(wp_plane[:].rearrange("p a i -> p (a i)").bitcast(I32), 0)
+
+        for q in range(QUADS):
+            nc.gpsimd.dma_start(
+                out=wp_plane[32 * q : 32 * q + 4, :, :].bitcast(I32),
+                in_=wp_scales[:, :, 4 * q : 4 * q + 4, :].rearrange("e s r i -> r (e s) i").bitcast(I32),
+            )
+        make_identity(nc, ident[:])
+
+        def load_x(s):
+            nc.sync.dma_start(out=x_win[s][:], in_=x_words[s].rearrange("p t d -> p (t d)").bitcast(I32))
+
+        raw = {}
+
+        def load_rows(name, rows):
+            width = rows.shape[1]
+            halves = raw.setdefault(name, [])
+            tile = held([P, PACK, width], F32, f"raw_{name}_{len(halves)}")
+            nc.sync.dma_start(out=tile[:], in_=rows.rearrange("(p j) w -> p j w", j=PACK))
+            for b in range(width // HALF):
+                halves.append(tile[:, :, b * HALF : (b + 1) * HALF])
+
+        def load_wp(e):
+            nc.sync.dma_start(
+                out=wp_sb[e][:].bitcast(I32), in_=wp_words[e].rearrange("s p b -> p s b").bitcast(I32)
+            )
+
+        nc.sync.dma_start(own_list[:], offs)
+        load_x(0)
+        nc.sync.dma_start(mate_list[:], offs2)
+        load_rows("w1_0_0", w1[0, 0:K_PASS, 0:HALF])
+        for q in range(QUADS):
+            nc.sync.dma_start(
+                out=both_win[32 * q : 32 * q + 8, :].bitcast(I32),
+                in_=x_scales[:, 4 * q : 4 * q + 4, :].bitcast(I32),
+            )
+        load_rows("w1_0_0", w1[0, 0:K_PASS, HALF:H])
+        load_x(1)
+        for q in range(QUADS):
+            nc.sync.dma_start(
+                out=last_win[32 * q : 32 * q + 4, :].bitcast(I32),
+                in_=x_scales[1, 4 * q : 4 * q + 4, :].bitcast(I32),
+            )
+        load_rows("w1_0_1", w1[0, K_PASS:K, :])
+        load_wp(0)
+        load_rows("w2_0", w2[0])
+        nc.sync.dma_start(out=gate_sb[:], in_=gate)
+        for e in range(1, E):
+            load_rows(f"w1_{e}_0", w1[e, 0:K_PASS, :])
+            load_wp(e)
+            load_rows(f"w1_{e}_1", w1[e, K_PASS:K, :])
+            load_rows(f"w2_{e}", w2[e])
+
+        own_words = [held([P, T], U32, f"own_words{s}") for s in range(PASSES)]
+        mate_words = [held([P, T], U32, f"mate_words{s}") for s in range(PASSES)]
+        own_scales = held([P, T], U8, "own_scales")
+        mate_scales = [held([P, T], U8, f"mate_scales{s}") for s in range(PASSES)]
+
+        def gather(lo, hi):
+            cols = slice(lo // 16, hi // 16)
+            for s in range(PASSES):
+                window = x_win[s][:].bitcast(U32)
+                nc.vector.tensor_copy(out=own_words[s][:, lo:hi], in_=window.indirect(own_list[:, cols]))
+                nc.vector.tensor_copy(out=mate_words[s][:, lo:hi], in_=window.indirect(mate_list[:, cols]))
+            nc.vector.tensor_copy(out=own_scales[:, lo:hi], in_=both_win[:].indirect(own_list[:, cols]))
+            nc.vector.tensor_copy(out=mate_scales[0][:, lo:hi], in_=both_win[:].indirect(mate_list[:, cols]))
+            nc.vector.tensor_copy(out=mate_scales[1][:, lo:hi], in_=last_win[:].indirect(mate_list[:, cols]))
+
+        def quantize_weight(name, calls):
+            grouped = held([P, H, PACK], BF16, f"grouped_{name}")
+            codes = held([P, H], U32, f"codes_{name}")
+            scales = held([P, H], U8, f"scales_{name}")
+            for b in range(2):
+                cols = slice(b * HALF, (b + 1) * HALF)
+                nc.scalar.copy(
+                    out=grouped[:, cols, :].rearrange("p (c i) t -> p c t i", i=LINE),
+                    in_=raw[name][b].rearrange("p t (c i) -> p c t i", i=LINE),
+                )
+            width = H // calls
+            for b in range(calls):
+                cols = slice(b * width, (b + 1) * width)
+                nc.vector.quantize_mx(
+                    out=codes[:, cols].bitcast(FP8X4),
+                    scales=scales[:, cols],
+                    in_=grouped[:, cols, :].rearrange("p c t -> p (c t)"),
+                )
+            return codes, scales
+
+        windows = [held([P, T], F32, f"window{n}") for n in range(N // P)]
+
+        def expert(e):
+            w1q = [quantize_weight(f"w1_{e}_{s}", 1) for s in range(PASSES)]
+            turned = psum.tile([P, C // P, 2, P], F32, name="turned", tag="turned", bufs=2)
+            for a in range(C // P):
+                slots = slice(e * C + a * P, e * C + (a + 1) * P)
+                acc = psum.tile([P, H], F32, name="acc", tag="acc", bufs=3)
+                for s in range(PASSES):
+                    nc.tensor.matmul_mx(
+                        out=acc[:],
+                        lhsT=mate_words[s][:, slots].bitcast(FP8X4),
+                        lhsT_scale=mate_scales[s][:, slots],
+                        rhs=wp_sb[e][:, s, :].bitcast(FP4X4),
+                        rhs_scale=wp_plane[:, e * PASSES + s, :],
+                        start=(s == 0),
+                        stop=False,
+                    )
+                for s in range(PASSES):
+                    nc.tensor.matmul_mx(
+                        out=acc[:],
+                        lhsT=own_words[s][:, slots].bitcast(FP8X4),
+                        lhsT_scale=own_scales[4 * s :, slots],
+                        rhs=w1q[s][0][:].bitcast(FP8X4),
+                        rhs_scale=w1q[s][1][:],
+                        start=False,
+                        stop=(s == PASSES - 1),
+                    )
+                h_rows = held([P, 2, P, 2], BF16, f"h_rows{e}_{a}")
+                nc.scalar.copy(out=h_rows[:], in_=acc[:].rearrange("s (p u v) -> s u p v", u=2, v=2))
+                pairs = h_rows[:].rearrange("s u p v -> s (u p v)").bitcast(F32)
+                for u in range(2):
+                    nc.tensor.transpose(turned[:, a, u, :], pairs[:, u * P : (u + 1) * P], ident[:])
+            w2_codes, w2_scales = quantize_weight(f"w2_{e}", 2)
+            h_grouped = held([P, C * PACK], BF16, f"h_grouped{e}")
+            nc.scalar.copy(
+                out=h_grouped[:].bitcast(F32).rearrange("p (a r u) -> p a r u", a=C // P, u=2),
+                in_=turned[:].rearrange("p a u r -> p a r u"),
+            )
+            h_codes = held([P, C], U32, f"h_codes{e}")
+            h_scales = held([P, C], U8, f"h_scales{e}")
+            nc.vector.quantize_mx(out=h_codes[:].bitcast(FP8X4), scales=h_scales[:], in_=h_grouped[:])
+            y_sb = []
+            for b in range(2):
+                y_bank = psum.tile([P, 2, C], F32, name="y_bank", tag="y_bank", bufs=3)
+                for c in range(2):
+                    cols = slice((2 * b + c) * P, (2 * b + c + 1) * P)
+                    nc.tensor.matmul_mx(
+                        out=y_bank[:, c, :],
+                        lhsT=w2_codes[:, cols].bitcast(FP8X4),
+                        lhsT_scale=w2_scales[:, cols],
+                        rhs=h_codes[:].bitcast(FP8X4),
+                        rhs_scale=h_scales[:],
+                        start=True,
+                        stop=True,
+                    )
+                y_pair = held([P, 2, C], F32, f"y_pair{e}_{b}")
+                nc.scalar.copy(out=y_pair[:], in_=y_bank[:])
+                y_sb.extend([y_pair[:, 0, :], y_pair[:, 1, :]])
+            return y_sb
+
+        def scatter(e, y_sb):
+            cols = slice(e * C // 16, (e + 1) * C // 16)
+            for n in range(N // P):
+                nc.vector.tensor_tensor(
+                    windows[n][:].indirect(own_list[:, cols]), y_sb[n], gate_sb[:, e * C : (e + 1) * C], MULT
+                )
+                if e == E - 1:
+                    nc.sync.dma_start(out=out[n * P : (n + 1) * P, :], in_=windows[n][:])
+
+        gather(0, C)
+        y0 = expert(0)
+        gather(C, T)
+        y1 = expert(1)
+        scatter(0, y0)
+        y2 = expert(2)
+        scatter(1, y1)
+        scatter(2, y2)

@@ -50,11 +50,6 @@ def tile_moe_duo_none_kernel(
         nc.vector.memset(last_win[:].bitcast(I32), 0)
         nc.vector.memset(wp_plane[:].rearrange("p a i -> p (a i)").bitcast(I32), 0)
 
-        for q in range(QUADS):
-            nc.gpsimd.dma_start(
-                out=wp_plane[32 * q : 32 * q + 4, :, :].bitcast(I32),
-                in_=wp_scales[:, :, 4 * q : 4 * q + 4, :].rearrange("e s r i -> r (e s) i").bitcast(I32),
-            )
         make_identity(nc, ident[:])
 
         def load_x(s):
@@ -93,28 +88,49 @@ def tile_moe_duo_none_kernel(
             )
         load_rows("w1_0_1", w1[0, K_PASS:K, :])
         load_wp(0)
+        for q in range(QUADS):
+            nc.sync.dma_start(
+                out=wp_plane[32 * q : 32 * q + 4, :, :].bitcast(I32),
+                in_=wp_scales[:, :, 4 * q : 4 * q + 4, :].rearrange("e s r i -> r (e s) i").bitcast(I32),
+            )
+        load_rows("w1_1_0", w1[1, 0:K_PASS, :])
         load_rows("w2_0", w2[0])
+        load_rows("w1_1_1", w1[1, K_PASS:K, :])
+        load_wp(1)
         nc.sync.dma_start(out=gate_sb[:], in_=gate)
-        for e in range(1, E):
-            load_rows(f"w1_{e}_0", w1[e, 0:K_PASS, :])
-            load_wp(e)
-            load_rows(f"w1_{e}_1", w1[e, K_PASS:K, :])
-            load_rows(f"w2_{e}", w2[e])
+        load_rows("w1_2_0", w1[2, 0:K_PASS, :])
+        load_rows("w2_1", w2[1])
+        load_rows("w1_2_1", w1[2, K_PASS:K, :])
+        load_wp(2)
+        load_rows("w2_2", w2[2])
 
-        own_words = [held([P, T], U32, f"own_words{s}") for s in range(PASSES)]
-        mate_words = [held([P, T], U32, f"mate_words{s}") for s in range(PASSES)]
-        own_scales = held([P, T], U8, "own_scales")
-        mate_scales = [held([P, T], U8, f"mate_scales{s}") for s in range(PASSES)]
+        own_words = [held([P, 2 * C], U32, f"own_words{s}") for s in range(PASSES)]
+        own_scales = held([P, 2 * C], U8, "own_scales")
+        mate_words = [held([P, C], U32, f"mate_words{s}") for s in range(PASSES)]
+        mate_scales = [held([P, C], U8, f"mate_scales{s}") for s in range(PASSES)]
+        windows = [held([P, T], F32, f"window{n}") for n in range(N // P)]
+        banks = [psum.tile([P, H], F32, name=f"bank{b}") for b in range(8)]
+        acc_bank = {(0, 0): 0, (0, 1): 1, (1, 0): 2, (1, 1): 3, (2, 0): 0, (2, 1): 1}
+        turn_bank = [4, 5, 4]
+        y_bank = {(0, 0): 6, (0, 1): 3, (1, 0): 7, (1, 1): 1, (2, 0): 6, (2, 1): 2}
 
-        def gather(lo, hi):
+        def gather_own(lo, hi):
             cols = slice(lo // 16, hi // 16)
+            dst = slice(lo % (2 * C), lo % (2 * C) + hi - lo)
             for s in range(PASSES):
                 window = x_win[s][:].bitcast(U32)
-                nc.vector.tensor_copy(out=own_words[s][:, lo:hi], in_=window.indirect(own_list[:, cols]))
-                nc.vector.tensor_copy(out=mate_words[s][:, lo:hi], in_=window.indirect(mate_list[:, cols]))
-            nc.vector.tensor_copy(out=own_scales[:, lo:hi], in_=both_win[:].indirect(own_list[:, cols]))
-            nc.vector.tensor_copy(out=mate_scales[0][:, lo:hi], in_=both_win[:].indirect(mate_list[:, cols]))
-            nc.vector.tensor_copy(out=mate_scales[1][:, lo:hi], in_=last_win[:].indirect(mate_list[:, cols]))
+                nc.vector.tensor_copy(out=own_words[s][:, dst], in_=window.indirect(own_list[:, cols]))
+            nc.vector.tensor_copy(out=own_scales[:, dst], in_=both_win[:].indirect(own_list[:, cols]))
+
+        def gather_mate(e):
+            cols = slice(e * C // 16, (e + 1) * C // 16)
+            for s in range(PASSES):
+                window = x_win[s][:].bitcast(U32)
+                nc.vector.tensor_copy(out=mate_words[s][:], in_=window.indirect(mate_list[:, cols]))
+            nc.vector.tensor_copy(out=mate_scales[0][:], in_=both_win[:].indirect(mate_list[:, cols]))
+            nc.vector.tensor_copy(out=mate_scales[1][:], in_=last_win[:].indirect(mate_list[:, cols]))
+
+        quantized = {}
 
         def quantize_weight(name, calls):
             grouped = held([P, H, PACK], BF16, f"grouped_{name}")
@@ -134,19 +150,14 @@ def tile_moe_duo_none_kernel(
                     scales=scales[:, cols],
                     in_=grouped[:, cols, :].rearrange("p c t -> p (c t)"),
                 )
-            return codes, scales
+            quantized[name] = (codes, scales)
 
-        windows = [held([P, T], F32, f"window{n}") for n in range(N // P)]
-
-        def expert(e):
-            w1q = [quantize_weight(f"w1_{e}_{s}", 1) for s in range(PASSES)]
-            turned = psum.tile([P, C // P, 2, P], F32, name="turned", tag="turned", bufs=2)
+        def first_layer(e):
             for a in range(C // P):
-                slots = slice(e * C + a * P, e * C + (a + 1) * P)
-                acc = psum.tile([P, H], F32, name="acc", tag="acc", bufs=3)
+                slots = slice(a * P, (a + 1) * P)
                 for s in range(PASSES):
                     nc.tensor.matmul_mx(
-                        out=acc[:],
+                        out=banks[acc_bank[e, a]][:],
                         lhsT=mate_words[s][:, slots].bitcast(FP8X4),
                         lhsT_scale=mate_scales[s][:, slots],
                         rhs=wp_sb[e][:, s, :].bitcast(FP4X4),
@@ -154,63 +165,95 @@ def tile_moe_duo_none_kernel(
                         start=(s == 0),
                         stop=False,
                     )
+            for a in range(C // P):
+                slots = slice((e % 2) * C + a * P, (e % 2) * C + (a + 1) * P)
                 for s in range(PASSES):
+                    codes, scales = quantized[f"w1_{e}_{s}"]
                     nc.tensor.matmul_mx(
-                        out=acc[:],
+                        out=banks[acc_bank[e, a]][:],
                         lhsT=own_words[s][:, slots].bitcast(FP8X4),
                         lhsT_scale=own_scales[4 * s :, slots],
-                        rhs=w1q[s][0][:].bitcast(FP8X4),
-                        rhs_scale=w1q[s][1][:],
+                        rhs=codes[:].bitcast(FP8X4),
+                        rhs_scale=scales[:],
                         start=False,
                         stop=(s == PASSES - 1),
                     )
+
+        def quantize_h(e):
+            turned = banks[turn_bank[e]][:].rearrange("p (a u r) -> p a u r", a=C // P, u=2)
+            for a in range(C // P):
                 h_rows = held([P, 2, P, 2], BF16, f"h_rows{e}_{a}")
-                nc.scalar.copy(out=h_rows[:], in_=acc[:].rearrange("s (p u v) -> s u p v", u=2, v=2))
+                nc.scalar.copy(
+                    out=h_rows[:], in_=banks[acc_bank[e, a]][:].rearrange("s (p u v) -> s u p v", u=2, v=2)
+                )
                 pairs = h_rows[:].rearrange("s u p v -> s (u p v)").bitcast(F32)
                 for u in range(2):
                     nc.tensor.transpose(turned[:, a, u, :], pairs[:, u * P : (u + 1) * P], ident[:])
-            w2_codes, w2_scales = quantize_weight(f"w2_{e}", 2)
             h_grouped = held([P, C * PACK], BF16, f"h_grouped{e}")
             nc.scalar.copy(
                 out=h_grouped[:].bitcast(F32).rearrange("p (a r u) -> p a r u", a=C // P, u=2),
-                in_=turned[:].rearrange("p a u r -> p a r u"),
+                in_=turned.rearrange("p a u r -> p a r u"),
             )
             h_codes = held([P, C], U32, f"h_codes{e}")
             h_scales = held([P, C], U8, f"h_scales{e}")
             nc.vector.quantize_mx(out=h_codes[:].bitcast(FP8X4), scales=h_scales[:], in_=h_grouped[:])
-            y_sb = []
-            for b in range(2):
-                y_bank = psum.tile([P, 2, C], F32, name="y_bank", tag="y_bank", bufs=3)
-                for c in range(2):
-                    cols = slice((2 * b + c) * P, (2 * b + c + 1) * P)
-                    nc.tensor.matmul_mx(
-                        out=y_bank[:, c, :],
-                        lhsT=w2_codes[:, cols].bitcast(FP8X4),
-                        lhsT_scale=w2_scales[:, cols],
-                        rhs=h_codes[:].bitcast(FP8X4),
-                        rhs_scale=h_scales[:],
-                        start=True,
-                        stop=True,
-                    )
-                y_pair = held([P, 2, C], F32, f"y_pair{e}_{b}")
-                nc.scalar.copy(out=y_pair[:], in_=y_bank[:])
-                y_sb.extend([y_pair[:, 0, :], y_pair[:, 1, :]])
-            return y_sb
+            quantized[f"h_{e}"] = (h_codes, h_scales)
 
-        def scatter(e, y_sb):
+        y_sb = {}
+
+        def second_layer(e, b):
+            w2_codes, w2_scales = quantized[f"w2_{e}"]
+            h_codes, h_scales = quantized[f"h_{e}"]
+            bank = banks[y_bank[e, b]]
+            for c in range(2):
+                cols = slice((2 * b + c) * P, (2 * b + c + 1) * P)
+                nc.tensor.matmul_mx(
+                    out=bank[:, c * C : (c + 1) * C],
+                    lhsT=w2_codes[:, cols].bitcast(FP8X4),
+                    lhsT_scale=w2_scales[:, cols],
+                    rhs=h_codes[:].bitcast(FP8X4),
+                    rhs_scale=h_scales[:],
+                    start=True,
+                    stop=True,
+                )
+            y_pair = held([P, 2 * C], F32, f"y_pair{e}_{b}")
+            nc.scalar.copy(out=y_pair[:], in_=bank[:])
+            y_sb[e, b] = y_pair
+
+        def scatter(e):
             cols = slice(e * C // 16, (e + 1) * C // 16)
             for n in range(N // P):
                 nc.vector.tensor_tensor(
-                    windows[n][:].indirect(own_list[:, cols]), y_sb[n], gate_sb[:, e * C : (e + 1) * C], MULT
+                    windows[n][:].indirect(own_list[:, cols]),
+                    y_sb[e, n // 2][:, (n % 2) * C : (n % 2 + 1) * C],
+                    gate_sb[:, e * C : (e + 1) * C],
+                    MULT,
                 )
                 if e == E - 1:
                     nc.sync.dma_start(out=out[n * P : (n + 1) * P, :], in_=windows[n][:])
 
-        gather(0, C)
-        y0 = expert(0)
-        gather(C, T)
-        y1 = expert(1)
-        scatter(0, y0)
-        y2 = expert(2)
-        scatter(1, y1)
-        scatter(2, y2)
+        gather_own(0, 2 * C)
+        gather_mate(0)
+        quantize_weight("w1_0_0", 1)
+        quantize_weight("w1_0_1", 1)
+        first_layer(0)
+        for e in range(E):
+            if e + 1 < E:
+                gather_mate(e + 1)
+            if e + 2 < E:
+                gather_own((e + 2) * C, (e + 3) * C)
+            if e == 0:
+                quantize_weight("w1_1_0", 1)
+            quantize_h(e)
+            if e > 0:
+                second_layer(e - 1, 1)
+            if e == 1:
+                quantize_weight("w1_2_0", 1)
+            quantize_weight(f"w2_{e}", 2)
+            if e + 1 < E:
+                quantize_weight(f"w1_{e + 1}_1", 1)
+                first_layer(e + 1)
+            second_layer(e, 0)
+        second_layer(E - 1, 1)
+        for e in range(E):
+            scatter(e)

@@ -15,6 +15,7 @@ U8 = mybir.dt.uint8
 FP8X4 = mybir.dt.float8_e4m3fn_x4
 FP4X4 = mybir.dt.float4_e2m1fn_x4
 MULT = mybir.AluOpType.mult
+ADD = mybir.AluOpType.add
 
 P = 128
 PACK = 4
@@ -22,7 +23,7 @@ K_PASS = P * PACK
 PASSES = K // K_PASS
 QUADS = 4
 HALF = 256
-LINE = 4
+LINE = 2
 
 
 def tile_moe_duo_none_kernel(
@@ -57,203 +58,299 @@ def tile_moe_duo_none_kernel(
 
         raw = {}
 
-        def load_rows(name, rows):
+        def load_rows(name, rows, first):
             width = rows.shape[1]
-            halves = raw.setdefault(name, [])
-            tile = held([P, PACK, width], F32, f"raw_{name}_{len(halves)}")
+            tile = held([P, PACK, width], F32, f"raw_{name}_{first}")
             nc.sync.dma_start(out=tile[:], in_=rows.rearrange("(p j) w -> p j w", j=PACK))
             for b in range(width // HALF):
-                halves.append(tile[:, :, b * HALF : (b + 1) * HALF])
+                raw[name, first + b] = tile[:, :, b * HALF : (b + 1) * HALF]
+
+        def load_both(q):
+            nc.sync.dma_start(
+                out=both_win[32 * q : 32 * q + 8, :].bitcast(I32),
+                in_=x_scales[:, 4 * q : 4 * q + 4, :].bitcast(I32),
+            )
+
+        def load_last(q):
+            nc.sync.dma_start(
+                out=last_win[32 * q : 32 * q + 4, :].bitcast(I32),
+                in_=x_scales[1, 4 * q : 4 * q + 4, :].bitcast(I32),
+            )
+
+        def load_plane(q):
+            nc.sync.dma_start(
+                out=wp_plane[32 * q : 32 * q + 4, :, :].bitcast(I32),
+                in_=wp_scales[:, :, 4 * q : 4 * q + 4, :].rearrange("e s r i -> r (e s) i").bitcast(I32),
+            )
 
         def load_wp(e):
             nc.sync.dma_start(
                 out=wp_sb[e][:].bitcast(I32), in_=wp_words[e].rearrange("s p b -> p s b").bitcast(I32)
             )
 
-        nc.sync.dma_start(own_list[:], offs)
         load_x(0)
-        nc.sync.dma_start(mate_list[:], offs2)
-        load_rows("w1_0_0", w1[0, 0:K_PASS, 0:HALF])
-        for q in range(QUADS):
-            nc.sync.dma_start(
-                out=both_win[32 * q : 32 * q + 8, :].bitcast(I32),
-                in_=x_scales[:, 4 * q : 4 * q + 4, :].bitcast(I32),
-            )
-        load_rows("w1_0_0", w1[0, 0:K_PASS, HALF:H])
         load_x(1)
-        for q in range(QUADS):
-            nc.sync.dma_start(
-                out=last_win[32 * q : 32 * q + 4, :].bitcast(I32),
-                in_=x_scales[1, 4 * q : 4 * q + 4, :].bitcast(I32),
-            )
-        load_rows("w1_0_1", w1[0, K_PASS:K, :])
+        nc.sync.dma_start(own_list[:], offs)
+        load_last(1)
+        load_both(1)
+        load_rows("w1_0_0", w1[0, 0:512, 0:HALF], 0)
+        nc.sync.dma_start(mate_list[:], offs2)
+        load_rows("w1_0_0", w1[0, 0:512, HALF:H], 1)
+        load_rows("w1_0_1", w1[0, 512:1024, :], 0)
+        load_both(0)
+        load_last(0)
+        load_plane(2)
+        load_both(2)
+        load_both(3)
+        load_last(2)
+        load_rows("w2_0", w2[0, :, :], 0)
+        load_last(3)
+        load_rows("w1_1_0", w1[1, 0:512, :], 0)
+        load_plane(0)
+        load_plane(3)
         load_wp(0)
-        for q in range(QUADS):
-            nc.sync.dma_start(
-                out=wp_plane[32 * q : 32 * q + 4, :, :].bitcast(I32),
-                in_=wp_scales[:, :, 4 * q : 4 * q + 4, :].rearrange("e s r i -> r (e s) i").bitcast(I32),
-            )
-        load_rows("w1_1_0", w1[1, 0:K_PASS, :])
-        load_rows("w2_0", w2[0])
-        load_rows("w1_1_1", w1[1, K_PASS:K, :])
-        load_wp(1)
+        load_plane(1)
+        load_rows("w1_1_1", w1[1, 512:1024, :], 0)
         nc.sync.dma_start(out=gate_sb[:], in_=gate)
-        load_rows("w1_2_0", w1[2, 0:K_PASS, :])
-        load_rows("w2_1", w2[1])
-        load_rows("w1_2_1", w1[2, K_PASS:K, :])
+        load_wp(1)
         load_wp(2)
-        load_rows("w2_2", w2[2])
+        load_rows("w1_2_0", w1[2, 0:512, :], 0)
+        load_rows("w2_1", w2[1, :, :], 0)
+        load_rows("w1_2_1", w1[2, 512:1024, :], 0)
+        load_rows("w2_2", w2[2, :, :], 0)
 
         own_words = [held([P, 2 * C], U32, f"own_words{s}") for s in range(PASSES)]
         own_scales = held([P, 2 * C], U8, "own_scales")
-        mate_words = [held([P, C], U32, f"mate_words{s}") for s in range(PASSES)]
-        mate_scales = [held([P, C], U8, f"mate_scales{s}") for s in range(PASSES)]
+        mate_words = [held([P, 2 * C], U32, f"mate_words{s}") for s in range(PASSES)]
+        mate_scales = [held([P, 2 * C], U8, f"mate_scales{s}") for s in range(PASSES)]
+        own_place = [0, 1, 0]
+        mate_place = [0, 1, 0]
         windows = [held([P, T], F32, f"window{n}") for n in range(N // P)]
         banks = [psum.tile([P, H], F32, name=f"bank{b}") for b in range(8)]
-        acc_bank = {(0, 0): 0, (0, 1): 1, (1, 0): 2, (1, 1): 3, (2, 0): 0, (2, 1): 1}
+        acc_bank = {(0, 0): 1, (0, 1): 0, (1, 0): 7, (1, 1): 2, (2, 0): 6, (2, 1): 1}
         turn_bank = [4, 5, 4]
-        y_bank = {(0, 0): 6, (0, 1): 3, (1, 0): 7, (1, 1): 1, (2, 0): 6, (2, 1): 2}
+        y_bank = {(0, 0): 1, (0, 1): 6, (1, 0): 0, (1, 1): 1, (2, 0): 2, (2, 1): 1}
 
-        def gather_own(lo, hi):
-            cols = slice(lo // 16, hi // 16)
-            dst = slice(lo % (2 * C), lo % (2 * C) + hi - lo)
-            for s in range(PASSES):
-                window = x_win[s][:].bitcast(U32)
-                nc.vector.tensor_copy(out=own_words[s][:, dst], in_=window.indirect(own_list[:, cols]))
-            nc.vector.tensor_copy(out=own_scales[:, dst], in_=both_win[:].indirect(own_list[:, cols]))
+        def gather(dst, place, window, offsets, e, count):
+            cols = slice(e * C // 16, (e + count) * C // 16)
+            nc.vector.tensor_copy(
+                out=dst[:, place[e] * C : (place[e] + count) * C], in_=window.indirect(offsets[:, cols])
+            )
 
-        def gather_mate(e):
-            cols = slice(e * C // 16, (e + 1) * C // 16)
-            for s in range(PASSES):
-                window = x_win[s][:].bitcast(U32)
-                nc.vector.tensor_copy(out=mate_words[s][:], in_=window.indirect(mate_list[:, cols]))
-            nc.vector.tensor_copy(out=mate_scales[0][:], in_=both_win[:].indirect(mate_list[:, cols]))
-            nc.vector.tensor_copy(out=mate_scales[1][:], in_=last_win[:].indirect(mate_list[:, cols]))
+        grouped, codes, scales = {}, {}, {}
+        for name in [f"w1_{e}_{s}" for e in range(E) for s in range(PASSES)] + [f"w2_{e}" for e in range(E)]:
+            grouped[name] = held([P, H, PACK], BF16, f"grouped_{name}")
+            codes[name] = held([P, H], U32, f"codes_{name}")
+            scales[name] = held([P, H], U8, f"scales_{name}")
 
-        quantized = {}
+        def cast(name, b):
+            nc.scalar.copy(
+                out=grouped[name][:, b * HALF : (b + 1) * HALF, :].rearrange("p (c i) t -> p c t i", i=LINE),
+                in_=raw[name, b].rearrange("p t (c i) -> p c t i", i=LINE),
+            )
 
-        def quantize_weight(name, calls):
-            grouped = held([P, H, PACK], BF16, f"grouped_{name}")
-            codes = held([P, H], U32, f"codes_{name}")
-            scales = held([P, H], U8, f"scales_{name}")
-            for b in range(2):
-                cols = slice(b * HALF, (b + 1) * HALF)
-                nc.scalar.copy(
-                    out=grouped[:, cols, :].rearrange("p (c i) t -> p c t i", i=LINE),
-                    in_=raw[name][b].rearrange("p t (c i) -> p c t i", i=LINE),
-                )
-            width = H // calls
-            for b in range(calls):
-                cols = slice(b * width, (b + 1) * width)
-                nc.vector.quantize_mx(
-                    out=codes[:, cols].bitcast(FP8X4),
-                    scales=scales[:, cols],
-                    in_=grouped[:, cols, :].rearrange("p c t -> p (c t)"),
-                )
-            quantized[name] = (codes, scales)
+        def cast_pool(name, b):
+            nc.gpsimd.tensor_scalar(
+                out=grouped[name][:, b * HALF : (b + 1) * HALF, :],
+                in0=raw[name, b].rearrange("p t c -> p c t"),
+                scalar1=1.0,
+                scalar2=0.0,
+                op0=MULT,
+                op1=ADD,
+            )
 
-        def first_layer(e):
-            for a in range(C // P):
-                slots = slice(a * P, (a + 1) * P)
-                for s in range(PASSES):
-                    nc.tensor.matmul_mx(
-                        out=banks[acc_bank[e, a]][:],
-                        lhsT=mate_words[s][:, slots].bitcast(FP8X4),
-                        lhsT_scale=mate_scales[s][:, slots],
-                        rhs=wp_sb[e][:, s, :].bitcast(FP4X4),
-                        rhs_scale=wp_plane[:, e * PASSES + s, :],
-                        start=(s == 0),
-                        stop=False,
-                    )
-            for a in range(C // P):
-                slots = slice((e % 2) * C + a * P, (e % 2) * C + (a + 1) * P)
-                for s in range(PASSES):
-                    codes, scales = quantized[f"w1_{e}_{s}"]
-                    nc.tensor.matmul_mx(
-                        out=banks[acc_bank[e, a]][:],
-                        lhsT=own_words[s][:, slots].bitcast(FP8X4),
-                        lhsT_scale=own_scales[4 * s :, slots],
-                        rhs=codes[:].bitcast(FP8X4),
-                        rhs_scale=scales[:],
-                        start=False,
-                        stop=(s == PASSES - 1),
-                    )
+        def quantize(name, lo, hi):
+            nc.vector.quantize_mx(
+                out=codes[name][:, lo:hi].bitcast(FP8X4),
+                scales=scales[name][:, lo:hi],
+                in_=grouped[name][:, lo:hi, :].rearrange("p c t -> p (c t)"),
+            )
+
+        passes_done = {}
+
+        def first_pass(e, a, lhsT, lhsT_scale, rhs, rhs_scale):
+            done = passes_done.get((e, a), 0)
+            nc.tensor.matmul_mx(
+                out=banks[acc_bank[e, a]][:],
+                lhsT=lhsT,
+                lhsT_scale=lhsT_scale,
+                rhs=rhs,
+                rhs_scale=rhs_scale,
+                start=(done == 0),
+                stop=(done == 2 * PASSES - 1),
+            )
+            passes_done[e, a] = done + 1
+
+        def mate_pass(e, a, s):
+            slots = slice(mate_place[e] * C + a * P, mate_place[e] * C + (a + 1) * P)
+            first_pass(
+                e, a, mate_words[s][:, slots].bitcast(FP8X4), mate_scales[s][:, slots],
+                wp_sb[e][:, s, :].bitcast(FP4X4), wp_plane[:, e * PASSES + s, :],
+            )
+
+        def own_pass(e, a, s):
+            slots = slice(own_place[e] * C + a * P, own_place[e] * C + (a + 1) * P)
+            name = f"w1_{e}_{s}"
+            first_pass(
+                e, a, own_words[s][:, slots].bitcast(FP8X4), own_scales[4 * s :, slots],
+                codes[name][:].bitcast(FP8X4), scales[name][:],
+            )
+
+        h_home = {}
+        y_home = {}
+
+        def turned(e):
+            return banks[turn_bank[e]][:].rearrange("p (a u r) -> p a u r", a=C // P, u=2)
+
+        def turn_h(e, a):
+            if (e, a) in h_home:
+                name, b, row = h_home[e, a]
+                pairs = raw[name, b][:, row, :]
+            else:
+                pairs = held([P, HALF], F32, f"h_rows{e}_{a}")[:]
+            nc.scalar.copy(
+                out=pairs.bitcast(BF16).rearrange("s (u p v) -> s u p v", u=2, v=2),
+                in_=banks[acc_bank[e, a]][:].rearrange("s (p u v) -> s u p v", u=2, v=2),
+            )
+            for u in range(2):
+                nc.tensor.transpose(turned(e)[:, a, u, :], pairs[:, u * P : (u + 1) * P], ident[:])
+
+        h_codes = [held([P, C], U32, f"h_codes{e}") for e in range(E)]
+        h_scales = [held([P, C], U8, f"h_scales{e}") for e in range(E)]
 
         def quantize_h(e):
-            turned = banks[turn_bank[e]][:].rearrange("p (a u r) -> p a u r", a=C // P, u=2)
-            for a in range(C // P):
-                h_rows = held([P, 2, P, 2], BF16, f"h_rows{e}_{a}")
-                nc.scalar.copy(
-                    out=h_rows[:], in_=banks[acc_bank[e, a]][:].rearrange("s (p u v) -> s u p v", u=2, v=2)
-                )
-                pairs = h_rows[:].rearrange("s u p v -> s (u p v)").bitcast(F32)
-                for u in range(2):
-                    nc.tensor.transpose(turned[:, a, u, :], pairs[:, u * P : (u + 1) * P], ident[:])
             h_grouped = held([P, C * PACK], BF16, f"h_grouped{e}")
             nc.scalar.copy(
                 out=h_grouped[:].bitcast(F32).rearrange("p (a r u) -> p a r u", a=C // P, u=2),
-                in_=turned.rearrange("p a u r -> p a r u"),
+                in_=turned(e).rearrange("p a u r -> p a r u"),
             )
-            h_codes = held([P, C], U32, f"h_codes{e}")
-            h_scales = held([P, C], U8, f"h_scales{e}")
-            nc.vector.quantize_mx(out=h_codes[:].bitcast(FP8X4), scales=h_scales[:], in_=h_grouped[:])
-            quantized[f"h_{e}"] = (h_codes, h_scales)
+            nc.vector.quantize_mx(out=h_codes[e][:].bitcast(FP8X4), scales=h_scales[e][:], in_=h_grouped[:])
 
         y_sb = {}
 
         def second_layer(e, b):
-            w2_codes, w2_scales = quantized[f"w2_{e}"]
-            h_codes, h_scales = quantized[f"h_{e}"]
             bank = banks[y_bank[e, b]]
             for c in range(2):
                 cols = slice((2 * b + c) * P, (2 * b + c + 1) * P)
                 nc.tensor.matmul_mx(
                     out=bank[:, c * C : (c + 1) * C],
-                    lhsT=w2_codes[:, cols].bitcast(FP8X4),
-                    lhsT_scale=w2_scales[:, cols],
-                    rhs=h_codes[:].bitcast(FP8X4),
-                    rhs_scale=h_scales[:],
+                    lhsT=codes[f"w2_{e}"][:, cols].bitcast(FP8X4),
+                    lhsT_scale=scales[f"w2_{e}"][:, cols],
+                    rhs=h_codes[e][:].bitcast(FP8X4),
+                    rhs_scale=h_scales[e][:],
                     start=True,
                     stop=True,
                 )
-            y_pair = held([P, 2 * C], F32, f"y_pair{e}_{b}")
-            nc.scalar.copy(out=y_pair[:], in_=bank[:])
+            if (e, b) in y_home:
+                name, half, row = y_home[e, b]
+                y_pair = raw[name, half][:, row : row + 2, :]
+            else:
+                y_pair = held([P, 2, C], F32, f"y_pair{e}_{b}")[:]
+            nc.scalar.copy(out=y_pair, in_=bank[:].rearrange("p (c j) -> p c j", c=2))
             y_sb[e, b] = y_pair
 
-        def scatter(e):
-            cols = slice(e * C // 16, (e + 1) * C // 16)
-            for n in range(N // P):
-                nc.vector.tensor_tensor(
-                    windows[n][:].indirect(own_list[:, cols]),
-                    y_sb[e, n // 2][:, (n % 2) * C : (n % 2 + 1) * C],
-                    gate_sb[:, e * C : (e + 1) * C],
-                    MULT,
-                )
-                if e == E - 1:
-                    nc.sync.dma_start(out=out[n * P : (n + 1) * P, :], in_=windows[n][:])
+        scattered = {}
 
-        gather_own(0, 2 * C)
-        gather_mate(0)
-        quantize_weight("w1_0_0", 1)
-        quantize_weight("w1_0_1", 1)
-        first_layer(0)
-        for e in range(E):
-            if e + 1 < E:
-                gather_mate(e + 1)
-            if e + 2 < E:
-                gather_own((e + 2) * C, (e + 3) * C)
-            if e == 0:
-                quantize_weight("w1_1_0", 1)
-            quantize_h(e)
-            if e > 0:
-                second_layer(e - 1, 1)
-            if e == 1:
-                quantize_weight("w1_2_0", 1)
-            quantize_weight(f"w2_{e}", 2)
-            if e + 1 < E:
-                quantize_weight(f"w1_{e + 1}_1", 1)
-                first_layer(e + 1)
-            second_layer(e, 0)
-        second_layer(E - 1, 1)
-        for e in range(E):
-            scatter(e)
+        def scatter(e, n):
+            nc.vector.tensor_tensor(
+                windows[n][:].indirect(own_list[:, e * C // 16 : (e + 1) * C // 16]),
+                y_sb[e, n // 2][:, n % 2, :],
+                gate_sb[:, e * C : (e + 1) * C],
+                MULT,
+            )
+            scattered[n] = scattered.get(n, 0) + 1
+            if scattered[n] == E:
+                nc.sync.dma_start(out=out[n * P : (n + 1) * P, :], in_=windows[n][:])
+
+        cast("w2_0", 1)
+        cast("w1_2_1", 0)
+        cast("w1_1_1", 1)
+        cast("w1_0_1", 0)
+        gather(own_scales, own_place, both_win[:], own_list, 0, 2)
+        gather(mate_scales[0], mate_place, both_win[:], mate_list, 0, 2)
+        cast("w1_0_0", 1)
+        gather(mate_scales[1], mate_place, last_win[:], mate_list, 0, 2)
+        gather(own_words[0], own_place, x_win[0][:].bitcast(U32), own_list, 0, 2)
+        cast("w1_0_0", 0)
+        gather(mate_words[1], mate_place, x_win[1][:].bitcast(U32), mate_list, 0, 2)
+        cast("w1_0_1", 1)
+        gather(mate_words[0], mate_place, x_win[0][:].bitcast(U32), mate_list, 0, 2)
+        mate_pass(0, 0, 0)
+        mate_pass(0, 1, 0)
+        cast("w1_1_0", 0)
+        quantize("w1_0_0", 0, H)
+        gather(own_words[1], own_place, x_win[1][:].bitcast(U32), own_list, 0, 2)
+        quantize("w1_0_1", 0, H)
+        mate_pass(1, 1, 1)
+        mate_pass(0, 1, 1)
+        cast("w2_0", 0)
+        own_pass(0, 0, 1)
+        cast("w1_1_0", 1)
+        own_pass(0, 1, 1)
+        own_pass(0, 0, 0)
+        quantize("w2_0", 0, H)
+        mate_pass(0, 0, 1)
+        gather(mate_scales[1], mate_place, last_win[:], mate_list, 2, 1)
+        mate_pass(1, 1, 0)
+        own_pass(0, 1, 0)
+        cast("w1_2_0", 1)
+        gather(mate_words[1], mate_place, x_win[1][:].bitcast(U32), mate_list, 2, 1)
+        gather(own_scales, own_place, both_win[:], own_list, 2, 1)
+        turn_h(0, 0)
+        quantize("w1_1_0", 0, H)
+        cast("w1_2_0", 0)
+        gather(mate_words[0], mate_place, x_win[0][:].bitcast(U32), mate_list, 2, 1)
+        gather(mate_scales[0], mate_place, both_win[:], mate_list, 2, 1)
+        turn_h(0, 1)
+        quantize_h(0)
+        cast("w1_1_1", 0)
+        quantize("w1_1_1", 0, H)
+        second_layer(0, 1)
+        mate_pass(1, 0, 0)
+        second_layer(0, 0)
+        own_pass(1, 0, 1)
+        gather(own_words[1], own_place, x_win[1][:].bitcast(U32), own_list, 2, 1)
+        cast("w2_1", 0)
+        mate_pass(1, 0, 1)
+        own_pass(1, 1, 0)
+        own_pass(1, 0, 0)
+        mate_pass(2, 0, 0)
+        turn_h(1, 0)
+        own_pass(1, 1, 1)
+        gather(own_words[0], own_place, x_win[0][:].bitcast(U32), own_list, 2, 1)
+        turn_h(1, 1)
+        scatter(0, 0)
+        quantize("w1_2_0", 0, H)
+        own_pass(2, 0, 0)
+        mate_pass(2, 1, 0)
+        mate_pass(2, 0, 1)
+        own_pass(2, 1, 0)
+        cast("w2_1", 1)
+        quantize_h(1)
+        scatter(0, 2)
+        cast("w1_2_1", 1)
+        scatter(0, 1)
+        quantize("w1_2_1", 0, H)
+        cast("w2_2", 0)
+        quantize("w2_1", 0, H)
+        own_pass(2, 1, 1)
+        cast("w2_2", 1)
+        own_pass(2, 0, 1)
+        scatter(0, 3)
+        second_layer(1, 0)
+        mate_pass(2, 1, 1)
+        turn_h(2, 0)
+        quantize("w2_2", 0, H)
+        scatter(1, 1)
+        turn_h(2, 1)
+        quantize_h(2)
+        scatter(1, 0)
+        second_layer(1, 1)
+        second_layer(2, 1)
+        scatter(1, 3)
+        second_layer(2, 0)
+        scatter(1, 2)
+        scatter(2, 0)
+        scatter(2, 3)
+        scatter(2, 2)
+        scatter(2, 1)

@@ -41,14 +41,14 @@ def tile_moe_duo_none_kernel(
         mate_list = keep.tile([P, T // 16], U16, name="mate_list")
         x_win = [held([P, T], I32, f"x_win{s}") for s in range(PASSES)]
         both_win = held([P, T], U8, "both_win")
-        last_win = held([P, T], U8, "last_win")
+        mate_scales = [held([P, T], U8, f"mate_scales{s}") for s in range(PASSES)]
         wp_plane = held([P, E * PASSES, H], U8, "wp_plane")
         wp_sb = [held([P, PASSES, 2 * H], U8, f"wp_sb{e}") for e in range(E)]
         gate_sb = held([P, T], F32, "gate_sb")
         ident = held([P, P], F32, "ident")
 
         nc.vector.memset(both_win[:].bitcast(I32), 0)
-        nc.vector.memset(last_win[:].bitcast(I32), 0)
+        nc.vector.memset(mate_scales[1][:].bitcast(I32), 0)
         nc.vector.memset(wp_plane[:].rearrange("p a i -> p (a i)").bitcast(I32), 0)
 
         make_identity(nc, ident[:])
@@ -71,12 +71,6 @@ def tile_moe_duo_none_kernel(
                 in_=x_scales[:, 4 * q : 4 * q + 4, :].bitcast(I32),
             )
 
-        def load_last(q):
-            nc.sync.dma_start(
-                out=last_win[32 * q : 32 * q + 4, :].bitcast(I32),
-                in_=x_scales[1, 4 * q : 4 * q + 4, :].bitcast(I32),
-            )
-
         def load_plane(q):
             nc.sync.dma_start(
                 out=wp_plane[32 * q : 32 * q + 4, :, :].bitcast(I32),
@@ -88,54 +82,53 @@ def tile_moe_duo_none_kernel(
                 out=wp_sb[e][:].bitcast(I32), in_=wp_words[e].rearrange("s p b -> p s b").bitcast(I32)
             )
 
-        load_x(0)
         load_x(1)
         nc.sync.dma_start(own_list[:], offs)
-        load_last(1)
-        load_both(1)
-        load_rows("w1_0_0", w1[0, 0:512, 0:HALF], 0)
         nc.sync.dma_start(mate_list[:], offs2)
-        load_rows("w1_0_0", w1[0, 0:512, HALF:H], 1)
+        load_both(2)
         load_rows("w1_0_1", w1[0, 512:1024, :], 0)
         load_both(0)
-        load_last(0)
-        load_plane(2)
-        load_both(2)
+        load_both(1)
         load_both(3)
-        load_last(2)
-        load_rows("w2_0", w2[0, :, :], 0)
-        load_last(3)
-        load_rows("w1_1_0", w1[1, 0:512, :], 0)
-        load_plane(0)
-        load_plane(3)
+        load_rows("w1_0_0", w1[0, 0:512, HALF:H], 1)
         load_wp(0)
+        load_rows("w2_0", w2[0, :, :], 0)
+        load_x(0)
+        load_plane(2)
+        load_rows("w1_0_0", w1[0, 0:512, 0:HALF], 0)
         load_plane(1)
         load_rows("w1_1_1", w1[1, 512:1024, :], 0)
-        nc.sync.dma_start(out=gate_sb[:], in_=gate)
-        load_wp(1)
-        load_wp(2)
+        load_plane(3)
+        load_plane(0)
+        load_rows("w1_1_0", w1[1, 0:512, :], 0)
         load_rows("w1_2_0", w1[2, 0:512, :], 0)
+        load_wp(1)
+        nc.sync.dma_start(out=gate_sb[:], in_=gate)
         load_rows("w2_1", w2[1, :, :], 0)
+        load_wp(2)
         load_rows("w1_2_1", w1[2, 512:1024, :], 0)
         load_rows("w2_2", w2[2, :, :], 0)
 
         own_words = [held([P, 2 * C], U32, f"own_words{s}") for s in range(PASSES)]
         own_scales = held([P, 2 * C], U8, "own_scales")
-        mate_words = [held([P, 2 * C], U32, f"mate_words{s}") for s in range(PASSES)]
-        mate_scales = [held([P, 2 * C], U8, f"mate_scales{s}") for s in range(PASSES)]
+        mate_words = [held([P, 1 * C], U32, f"mate_words{s}") for s in range(PASSES)]
+        every_place = [0, 1, 2]
         own_place = [0, 1, 0]
-        mate_place = [0, 1, 0]
+        mate_place = [0, 0, 0]
         windows = [held([P, T], F32, f"window{n}") for n in range(N // P)]
         banks = [psum.tile([P, H], F32, name=f"bank{b}") for b in range(8)]
-        acc_bank = {(0, 0): 1, (0, 1): 0, (1, 0): 7, (1, 1): 2, (2, 0): 6, (2, 1): 1}
+        acc_bank = {(0, 0): 2, (0, 1): 0, (1, 0): 3, (1, 1): 6, (2, 0): 1, (2, 1): 7}
         turn_bank = [4, 5, 4]
-        y_bank = {(0, 0): 1, (0, 1): 6, (1, 0): 0, (1, 1): 1, (2, 0): 2, (2, 1): 1}
+        y_bank = {(0, 0): 2, (0, 1): 0, (1, 0): 2, (1, 1): 1, (2, 0): 6, (2, 1): 3}
 
         def gather(dst, place, window, offsets, e, count):
             cols = slice(e * C // 16, (e + count) * C // 16)
             nc.vector.tensor_copy(
                 out=dst[:, place[e] * C : (place[e] + count) * C], in_=window.indirect(offsets[:, cols])
             )
+
+        def move_mate_scales():
+            nc.gpsimd.dma_start(out=mate_scales[1][0:100, :].bitcast(I32), in_=mate_scales[0][4:104, :].bitcast(I32))
 
         grouped, codes, scales = {}, {}, {}
         for name in [f"w1_{e}_{s}" for e in range(E) for s in range(PASSES)] + [f"w2_{e}" for e in range(E)]:
@@ -145,6 +138,12 @@ def tile_moe_duo_none_kernel(
 
         def cast(name, b):
             nc.scalar.copy(
+                out=grouped[name][:, b * HALF : (b + 1) * HALF, :].rearrange("p (c i) t -> p c t i", i=LINE),
+                in_=raw[name, b].rearrange("p t (c i) -> p c t i", i=LINE),
+            )
+
+        def cast_vector(name, b):
+            nc.vector.tensor_copy(
                 out=grouped[name][:, b * HALF : (b + 1) * HALF, :].rearrange("p (c i) t -> p c t i", i=LINE),
                 in_=raw[name, b].rearrange("p t (c i) -> p c t i", i=LINE),
             )
@@ -184,7 +183,7 @@ def tile_moe_duo_none_kernel(
         def mate_pass(e, a, s):
             slots = slice(mate_place[e] * C + a * P, mate_place[e] * C + (a + 1) * P)
             first_pass(
-                e, a, mate_words[s][:, slots].bitcast(FP8X4), mate_scales[s][:, slots],
+                e, a, mate_words[s][:, slots].bitcast(FP8X4), mate_scales[s][:, e * C + a * P : e * C + (a + 1) * P],
                 wp_sb[e][:, s, :].bitcast(FP4X4), wp_plane[:, e * PASSES + s, :],
             )
 
@@ -197,7 +196,7 @@ def tile_moe_duo_none_kernel(
             )
 
         h_home = {}
-        y_home = {}
+        y_home = {(0, 1): ("w1_2_1", 1, 0), (1, 0): ("w1_2_1", 1, 2)}
 
         def turned(e):
             return banks[turn_bank[e]][:].rearrange("p (a u r) -> p a u r", a=C // P, u=2)
@@ -262,95 +261,96 @@ def tile_moe_duo_none_kernel(
             if scattered[n] == E:
                 nc.sync.dma_start(out=out[n * P : (n + 1) * P, :], in_=windows[n][:])
 
-        cast("w2_0", 1)
-        cast("w1_2_1", 0)
-        cast("w1_1_1", 1)
-        cast("w1_0_1", 0)
-        gather(own_scales, own_place, both_win[:], own_list, 0, 2)
-        gather(mate_scales[0], mate_place, both_win[:], mate_list, 0, 2)
-        cast("w1_0_0", 1)
-        gather(mate_scales[1], mate_place, last_win[:], mate_list, 0, 2)
-        gather(own_words[0], own_place, x_win[0][:].bitcast(U32), own_list, 0, 2)
-        cast("w1_0_0", 0)
-        gather(mate_words[1], mate_place, x_win[1][:].bitcast(U32), mate_list, 0, 2)
         cast("w1_0_1", 1)
-        gather(mate_words[0], mate_place, x_win[0][:].bitcast(U32), mate_list, 0, 2)
+        cast("w1_0_0", 0)
+        cast("w1_1_1", 1)
+        cast_vector("w2_1", 0)
+        gather(mate_words[1], mate_place, x_win[1][:].bitcast(U32), mate_list, 0, 1)
+        gather(mate_scales[0], every_place, both_win[:], mate_list, 2, 1)
+        gather(mate_words[0], mate_place, x_win[0][:].bitcast(U32), mate_list, 0, 1)
+        gather(mate_scales[0], every_place, both_win[:], mate_list, 0, 2)
+        gather(own_words[0], own_place, x_win[0][:].bitcast(U32), own_list, 0, 2)
+        cast_vector("w1_0_0", 1)
+        cast("w1_0_1", 0)
+        cast_vector("w1_2_0", 0)
+        move_mate_scales()
+        quantize("w1_0_0", 0, H)
+        quantize("w1_0_1", 0, H)
         mate_pass(0, 0, 0)
         mate_pass(0, 1, 0)
-        cast("w1_1_0", 0)
-        quantize("w1_0_0", 0, H)
-        gather(own_words[1], own_place, x_win[1][:].bitcast(U32), own_list, 0, 2)
-        quantize("w1_0_1", 0, H)
-        mate_pass(1, 1, 1)
-        mate_pass(0, 1, 1)
-        cast("w2_0", 0)
-        own_pass(0, 0, 1)
-        cast("w1_1_0", 1)
-        own_pass(0, 1, 1)
-        own_pass(0, 0, 0)
-        quantize("w2_0", 0, H)
         mate_pass(0, 0, 1)
-        gather(mate_scales[1], mate_place, last_win[:], mate_list, 2, 1)
-        mate_pass(1, 1, 0)
-        own_pass(0, 1, 0)
-        cast("w1_2_0", 1)
-        gather(mate_words[1], mate_place, x_win[1][:].bitcast(U32), mate_list, 2, 1)
-        gather(own_scales, own_place, both_win[:], own_list, 2, 1)
-        turn_h(0, 0)
-        quantize("w1_1_0", 0, H)
-        cast("w1_2_0", 0)
-        gather(mate_words[0], mate_place, x_win[0][:].bitcast(U32), mate_list, 2, 1)
-        gather(mate_scales[0], mate_place, both_win[:], mate_list, 2, 1)
-        turn_h(0, 1)
-        quantize_h(0)
+        gather(mate_words[0], mate_place, x_win[0][:].bitcast(U32), mate_list, 1, 1)
+        mate_pass(0, 1, 1)
+        gather(mate_words[1], mate_place, x_win[1][:].bitcast(U32), mate_list, 1, 1)
         cast("w1_1_1", 0)
+        mate_pass(1, 1, 0)
+        gather(own_words[1], own_place, x_win[1][:].bitcast(U32), own_list, 0, 2)
+        gather(own_scales, own_place, both_win[:], own_list, 0, 2)
         quantize("w1_1_1", 0, H)
-        second_layer(0, 1)
-        mate_pass(1, 0, 0)
-        second_layer(0, 0)
+        cast("w1_1_0", 0)
+        own_pass(0, 1, 1)
         own_pass(1, 0, 1)
-        gather(own_words[1], own_place, x_win[1][:].bitcast(U32), own_list, 2, 1)
-        cast("w2_1", 0)
-        mate_pass(1, 0, 1)
-        own_pass(1, 1, 0)
-        own_pass(1, 0, 0)
-        mate_pass(2, 0, 0)
-        turn_h(1, 0)
-        own_pass(1, 1, 1)
-        gather(own_words[0], own_place, x_win[0][:].bitcast(U32), own_list, 2, 1)
-        turn_h(1, 1)
-        scatter(0, 0)
-        quantize("w1_2_0", 0, H)
-        own_pass(2, 0, 0)
-        mate_pass(2, 1, 0)
-        mate_pass(2, 0, 1)
-        own_pass(2, 1, 0)
-        cast("w2_1", 1)
-        quantize_h(1)
-        scatter(0, 2)
+        mate_pass(1, 0, 0)
+        own_pass(0, 0, 1)
         cast("w1_2_1", 1)
-        scatter(0, 1)
+        mate_pass(1, 0, 1)
+        cast_vector("w1_2_0", 1)
+        cast("w2_0", 0)
+        cast_vector("w2_1", 1)
+        own_pass(0, 1, 0)
+        cast("w1_2_1", 0)
+        turn_h(0, 1)
+        own_pass(0, 0, 0)
+        gather(own_words[1], own_place, x_win[1][:].bitcast(U32), own_list, 2, 1)
+        cast("w2_0", 1)
+        turn_h(0, 0)
+        cast("w1_1_0", 1)
+        own_pass(1, 1, 1)
+        mate_pass(1, 1, 1)
+        quantize("w1_1_0", 0, H)
+        gather(mate_words[0], mate_place, x_win[0][:].bitcast(U32), mate_list, 2, 1)
         quantize("w1_2_1", 0, H)
-        cast("w2_2", 0)
-        quantize("w2_1", 0, H)
-        own_pass(2, 1, 1)
+        own_pass(1, 0, 0)
+        quantize("w2_0", 0, H)
+        own_pass(1, 1, 0)
+        quantize_h(0)
+        quantize("w1_2_0", 0, H)
+        second_layer(0, 1)
+        gather(mate_words[1], mate_place, x_win[1][:].bitcast(U32), mate_list, 2, 1)
+        second_layer(0, 0)
         cast("w2_2", 1)
-        own_pass(2, 0, 1)
-        scatter(0, 3)
-        second_layer(1, 0)
+        quantize("w2_1", 0, H)
+        scatter(0, 1)
+        gather(own_scales, own_place, both_win[:], own_list, 2, 1)
+        gather(own_words[0], own_place, x_win[0][:].bitcast(U32), own_list, 2, 1)
+        scatter(0, 0)
         mate_pass(2, 1, 1)
-        turn_h(2, 0)
+        turn_h(1, 0)
+        cast("w2_2", 0)
+        own_pass(2, 0, 1)
+        own_pass(2, 1, 0)
+        mate_pass(2, 0, 1)
         quantize("w2_2", 0, H)
-        scatter(1, 1)
-        turn_h(2, 1)
-        quantize_h(2)
+        mate_pass(2, 0, 0)
+        turn_h(1, 1)
+        own_pass(2, 1, 1)
+        quantize_h(1)
+        second_layer(1, 0)
         scatter(1, 0)
+        mate_pass(2, 1, 0)
+        turn_h(2, 1)
+        own_pass(2, 0, 0)
+        turn_h(2, 0)
+        quantize_h(2)
         second_layer(1, 1)
-        second_layer(2, 1)
+        scatter(0, 3)
         scatter(1, 3)
         second_layer(2, 0)
+        scatter(0, 2)
+        second_layer(2, 1)
+        scatter(1, 1)
         scatter(1, 2)
         scatter(2, 0)
-        scatter(2, 3)
-        scatter(2, 2)
         scatter(2, 1)
+        scatter(2, 2)
+        scatter(2, 3)

@@ -15,14 +15,12 @@ U8 = mybir.dt.uint8
 FP8X4 = mybir.dt.float8_e4m3fn_x4
 FP4X4 = mybir.dt.float4_e2m1fn_x4
 MULT = mybir.AluOpType.mult
-ADD = mybir.AluOpType.add
 
 P = 128
 PACK = 4
 K_PASS = P * PACK
 PASSES = K // K_PASS
 QUADS = 4
-HALF = 256
 LINE = 2
 
 
@@ -34,205 +32,160 @@ def tile_moe_duo_none_kernel(
         keep = ctx.enter_context(tc.tile_pool(name="keep", bufs=1))
         psum = ctx.enter_context(tc.psum_pool(name="psum", bufs=1))
 
-        def held(shape, dtype, name):
-            return keep.tile(shape, dtype, name=name, align_bytes=64)
+        def held(shape, dtype, name, tag=None):
+            return keep.tile(shape, dtype, name=name, tag=tag or name, align_bytes=64)
 
         own_list = keep.tile([P, T // 16], U16, name="own_list")
         mate_list = keep.tile([P, T // 16], U16, name="mate_list")
         x_win = [held([P, T], I32, f"x_win{s}") for s in range(PASSES)]
-        both_win = held([P, T], U8, "both_win")
+        scale_win = held([P, T], U8, "scale_win")
+        own_scales = held([P, T], U8, "own_scales")
         mate_scales = [held([P, T], U8, f"mate_scales{s}") for s in range(PASSES)]
         wp_plane = held([P, E * PASSES, H], U8, "wp_plane")
         wp_sb = [held([P, PASSES, 2 * H], U8, f"wp_sb{e}") for e in range(E)]
         gate_sb = held([P, T], F32, "gate_sb")
         ident = held([P, P], F32, "ident")
 
-        nc.vector.memset(both_win[:].bitcast(I32), 0)
-        nc.vector.memset(mate_scales[1][:].bitcast(I32), 0)
+        nc.vector.memset(scale_win[:].bitcast(I32), 0)
         nc.vector.memset(wp_plane[:].rearrange("p a i -> p (a i)").bitcast(I32), 0)
-
+        nc.vector.memset(mate_scales[1][:].bitcast(I32), 0)
         make_identity(nc, ident[:])
+
+        raw = {}
 
         def load_x(s):
             nc.sync.dma_start(out=x_win[s][:], in_=x_words[s].rearrange("p t d -> p (t d)").bitcast(I32))
 
-        raw = {}
+        def load_matrix(name, rows):
+            raw[name] = held([P, PACK, H], F32, f"raw_{name}")
+            nc.sync.dma_start(out=raw[name][:], in_=rows.rearrange("(p j) w -> p j w", j=PACK))
 
-        def load_rows(name, rows, first):
-            width = rows.shape[1]
-            tile = held([P, PACK, width], F32, f"raw_{name}_{first}")
-            nc.sync.dma_start(out=tile[:], in_=rows.rearrange("(p j) w -> p j w", j=PACK))
-            for b in range(width // HALF):
-                raw[name, first + b] = tile[:, :, b * HALF : (b + 1) * HALF]
-
-        def load_both(q):
-            nc.sync.dma_start(
-                out=both_win[32 * q : 32 * q + 8, :].bitcast(I32),
-                in_=x_scales[:, 4 * q : 4 * q + 4, :].bitcast(I32),
-            )
-
-        def load_plane(q):
-            nc.sync.dma_start(
-                out=wp_plane[32 * q : 32 * q + 4, :, :].bitcast(I32),
-                in_=wp_scales[:, :, 4 * q : 4 * q + 4, :].rearrange("e s r i -> r (e s) i").bitcast(I32),
-            )
+        def load_w1(e, s):
+            load_matrix(f"w1_{e}_{s}", w1[e, s * K_PASS : (s + 1) * K_PASS, :])
 
         def load_wp(e):
             nc.sync.dma_start(
                 out=wp_sb[e][:].bitcast(I32), in_=wp_words[e].rearrange("s p b -> p s b").bitcast(I32)
             )
 
-        load_x(1)
-        nc.sync.dma_start(own_list[:], offs)
         nc.sync.dma_start(mate_list[:], offs2)
-        load_both(2)
-        load_rows("w1_0_1", w1[0, 512:1024, :], 0)
-        load_both(0)
-        load_both(1)
-        load_both(3)
-        load_rows("w1_0_0", w1[0, 0:512, HALF:H], 1)
-        load_wp(0)
-        load_rows("w2_0", w2[0, :, :], 0)
+        nc.sync.dma_start(own_list[:], offs)
+        for q in range(QUADS):
+            nc.sync.dma_start(
+                out=scale_win[32 * q : 32 * q + 8, :].bitcast(I32),
+                in_=x_scales[:, 4 * q : 4 * q + 4, :].bitcast(I32),
+            )
         load_x(0)
-        load_plane(2)
-        load_rows("w1_0_0", w1[0, 0:512, 0:HALF], 0)
-        load_plane(1)
-        load_rows("w1_1_1", w1[1, 512:1024, :], 0)
-        load_plane(3)
-        load_plane(0)
-        load_rows("w1_1_0", w1[1, 0:512, :], 0)
-        load_rows("w1_2_0", w1[2, 0:512, :], 0)
-        load_wp(1)
-        nc.sync.dma_start(out=gate_sb[:], in_=gate)
-        load_rows("w2_1", w2[1, :, :], 0)
-        load_wp(2)
-        load_rows("w1_2_1", w1[2, 512:1024, :], 0)
-        load_rows("w2_2", w2[2, :, :], 0)
-
-        own_words = [held([P, 2 * C], U32, f"own_words{s}") for s in range(PASSES)]
-        own_scales = held([P, 2 * C], U8, "own_scales")
-        mate_words = [held([P, 1 * C], U32, f"mate_words{s}") for s in range(PASSES)]
-        every_place = [0, 1, 2]
-        own_place = [0, 1, 0]
-        mate_place = [0, 0, 0]
-        windows = [held([P, T], F32, f"window{n}") for n in range(N // P)]
-        banks = [psum.tile([P, H], F32, name=f"bank{b}") for b in range(8)]
-        acc_bank = {(0, 0): 2, (0, 1): 0, (1, 0): 3, (1, 1): 6, (2, 0): 1, (2, 1): 7}
-        turn_bank = [4, 5, 4]
-        y_bank = {(0, 0): 2, (0, 1): 0, (1, 0): 2, (1, 1): 1, (2, 0): 6, (2, 1): 3}
-
-        def gather(dst, place, window, offsets, e, count):
-            cols = slice(e * C // 16, (e + count) * C // 16)
-            nc.vector.tensor_copy(
-                out=dst[:, place[e] * C : (place[e] + count) * C], in_=window.indirect(offsets[:, cols])
+        load_w1(0, 0)
+        load_w1(0, 1)
+        load_wp(0)
+        for q in range(QUADS):
+            nc.sync.dma_start(
+                out=wp_plane[32 * q : 32 * q + 4, :, :].bitcast(I32),
+                in_=wp_scales[:, :, 4 * q : 4 * q + 4, :].rearrange("e s r i -> r (e s) i").bitcast(I32),
             )
 
-        def move_mate_scales():
-            nc.gpsimd.dma_start(out=mate_scales[1][0:100, :].bitcast(I32), in_=mate_scales[0][4:104, :].bitcast(I32))
+        def gather(dst, window, offsets, first, count):
+            nc.vector.tensor_copy(out=dst, in_=window.indirect(offsets[:, first // 16 : (first + count) // 16]))
 
-        grouped, codes, scales = {}, {}, {}
-        for name in [f"w1_{e}_{s}" for e in range(E) for s in range(PASSES)] + [f"w2_{e}" for e in range(E)]:
-            grouped[name] = held([P, H, PACK], BF16, f"grouped_{name}")
-            codes[name] = held([P, H], U32, f"codes_{name}")
+        for first, count in ((0, 2 * C), (2 * C, C)):
+            gather(mate_scales[0][:, first : first + count], scale_win[:], mate_list, first, count)
+        nc.sync.dma_start(out=mate_scales[1][0:100, :].bitcast(I32), in_=mate_scales[0][4:104, :].bitcast(I32))
+        for first, count in ((0, 2 * C), (2 * C, C)):
+            gather(own_scales[:, first : first + count], scale_win[:], own_list, first, count)
+
+        load_x(1)
+        load_matrix("w2_0", w2[0])
+        for e in range(1, E):
+            load_w1(e, 0)
+            load_w1(e, 1)
+            if e == 1:
+                nc.sync.dma_start(out=gate_sb[:], in_=gate)
+            load_wp(e)
+            load_matrix(f"w2_{e}", w2[e])
+
+        codes, scales = {}, {}
+
+        def quantize_matrix(name, home=None, vector_from=H, codes_home=None, pieces=1):
+            grouped = held([P, H, PACK], BF16, f"grouped_{name}", home)
+            dst = grouped[:].rearrange("p (c i) t -> p c t i", i=LINE)
+            src = raw[name][:].rearrange("p t (c i) -> p c t i", i=LINE)
+            width = vector_from // LINE // pieces
+            for piece in range(pieces if vector_from > 0 else 0):
+                cols = slice(piece * width, (piece + 1) * width)
+                nc.scalar.copy(out=dst[:, cols], in_=src[:, cols])
+            if vector_from < H:
+                nc.vector.tensor_copy(out=dst[:, vector_from // LINE :], in_=src[:, vector_from // LINE :])
+            codes[name] = held([P, H], U32, f"codes_{name}", codes_home)
             scales[name] = held([P, H], U8, f"scales_{name}")
-
-        def cast(name, b):
-            nc.scalar.copy(
-                out=grouped[name][:, b * HALF : (b + 1) * HALF, :].rearrange("p (c i) t -> p c t i", i=LINE),
-                in_=raw[name, b].rearrange("p t (c i) -> p c t i", i=LINE),
-            )
-
-        def cast_vector(name, b):
-            nc.vector.tensor_copy(
-                out=grouped[name][:, b * HALF : (b + 1) * HALF, :].rearrange("p (c i) t -> p c t i", i=LINE),
-                in_=raw[name, b].rearrange("p t (c i) -> p c t i", i=LINE),
-            )
-
-        def cast_pool(name, b):
-            nc.gpsimd.tensor_scalar(
-                out=grouped[name][:, b * HALF : (b + 1) * HALF, :],
-                in0=raw[name, b].rearrange("p t c -> p c t"),
-                scalar1=1.0,
-                scalar2=0.0,
-                op0=MULT,
-                op1=ADD,
-            )
-
-        def quantize(name, lo, hi):
             nc.vector.quantize_mx(
-                out=codes[name][:, lo:hi].bitcast(FP8X4),
-                scales=scales[name][:, lo:hi],
-                in_=grouped[name][:, lo:hi, :].rearrange("p c t -> p (c t)"),
+                out=codes[name][:].bitcast(FP8X4),
+                scales=scales[name][:],
+                in_=grouped[:].rearrange("p c t -> p (c t)"),
             )
 
-        passes_done = {}
+        windows = {}
+        words, acc, turn, h_codes, h_scales, y_sb = {}, {}, {}, {}, {}, {}
 
-        def first_pass(e, a, lhsT, lhsT_scale, rhs, rhs_scale):
-            done = passes_done.get((e, a), 0)
-            nc.tensor.matmul_mx(
-                out=banks[acc_bank[e, a]][:],
-                lhsT=lhsT,
-                lhsT_scale=lhsT_scale,
-                rhs=rhs,
-                rhs_scale=rhs_scale,
-                start=(done == 0),
-                stop=(done == 2 * PASSES - 1),
-            )
-            passes_done[e, a] = done + 1
+        def gather_words(kind, first, count, s, home=None):
+            tile = held([P, count * C], U32, f"words_{kind}{first}_{s}", home)
+            gather(tile[:], x_win[s][:].bitcast(U32), mate_list if kind == "mate" else own_list, first * C, count * C)
+            for e in range(count):
+                words[kind, first + e, s] = tile[:, e * C : (e + 1) * C]
 
-        def mate_pass(e, a, s):
-            slots = slice(mate_place[e] * C + a * P, mate_place[e] * C + (a + 1) * P)
-            first_pass(
-                e, a, mate_words[s][:, slots].bitcast(FP8X4), mate_scales[s][:, e * C + a * P : e * C + (a + 1) * P],
-                wp_sb[e][:, s, :].bitcast(FP4X4), wp_plane[:, e * PASSES + s, :],
-            )
+        def first_layer(e, order):
+            for a in range(C // P):
+                acc[e, a] = psum.tile([P, H], F32, name=f"acc{e}_{a}", tag=f"acc{a}")
+            for step, (kind, s) in enumerate(order + [("own", 1)]):
+                for a in range(C // P):
+                    here = slice(a * P, (a + 1) * P)
+                    slots = slice(e * C + a * P, e * C + (a + 1) * P)
+                    if kind == "mate":
+                        lhsT, lhsT_scale = words[kind, e, s][:, here], mate_scales[s][:, slots]
+                        rhs, rhs_scale = wp_sb[e][:, s, :].bitcast(FP4X4), wp_plane[:, e * PASSES + s, :]
+                    else:
+                        lhsT, lhsT_scale = words[kind, e, s][:, here], own_scales[4 * s :, slots]
+                        rhs, rhs_scale = codes[f"w1_{e}_{s}"][:].bitcast(FP8X4), scales[f"w1_{e}_{s}"][:]
+                    nc.tensor.matmul_mx(
+                        out=acc[e, a][:],
+                        lhsT=lhsT.bitcast(FP8X4),
+                        lhsT_scale=lhsT_scale,
+                        rhs=rhs,
+                        rhs_scale=rhs_scale,
+                        start=(step == 0),
+                        stop=(kind == "own" and s == PASSES - 1),
+                    )
 
-        def own_pass(e, a, s):
-            slots = slice(own_place[e] * C + a * P, own_place[e] * C + (a + 1) * P)
-            name = f"w1_{e}_{s}"
-            first_pass(
-                e, a, own_words[s][:, slots].bitcast(FP8X4), own_scales[4 * s :, slots],
-                codes[name][:].bitcast(FP8X4), scales[name][:],
-            )
+        def turn_h(e, home):
+            turn[e] = psum.tile([P, C // P, 2, P], F32, name=f"turn{e}", tag=f"turn{e % 2}")
+            for a in range(C // P):
+                if home is None:
+                    pairs = held([P, H // 2], F32, f"h_rows{e}_{a}")[:]
+                else:
+                    pairs = raw[home][:, a, 0 : H // 2]
+                nc.scalar.copy(
+                    out=pairs.bitcast(BF16).rearrange("s (u p v) -> s u p v", u=2, v=2),
+                    in_=acc[e, a][:].rearrange("s (p u v) -> s u p v", u=2, v=2),
+                )
+                for u in range(2):
+                    nc.tensor.transpose(turn[e][:, a, u, :], pairs[:, u * P : (u + 1) * P], ident[:])
 
-        h_home = {}
-        y_home = {(0, 1): ("w1_2_1", 1, 0), (1, 0): ("w1_2_1", 1, 2)}
-
-        def turned(e):
-            return banks[turn_bank[e]][:].rearrange("p (a u r) -> p a u r", a=C // P, u=2)
-
-        def turn_h(e, a):
-            if (e, a) in h_home:
-                name, b, row = h_home[e, a]
-                pairs = raw[name, b][:, row, :]
-            else:
-                pairs = held([P, HALF], F32, f"h_rows{e}_{a}")[:]
-            nc.scalar.copy(
-                out=pairs.bitcast(BF16).rearrange("s (u p v) -> s u p v", u=2, v=2),
-                in_=banks[acc_bank[e, a]][:].rearrange("s (p u v) -> s u p v", u=2, v=2),
-            )
-            for u in range(2):
-                nc.tensor.transpose(turned(e)[:, a, u, :], pairs[:, u * P : (u + 1) * P], ident[:])
-
-        h_codes = [held([P, C], U32, f"h_codes{e}") for e in range(E)]
-        h_scales = [held([P, C], U8, f"h_scales{e}") for e in range(E)]
-
-        def quantize_h(e):
-            h_grouped = held([P, C * PACK], BF16, f"h_grouped{e}")
+        def quantize_h(e, home, codes_home=None):
+            h_grouped = held([P, C * PACK], BF16, f"h_grouped{e}", home)
             nc.scalar.copy(
                 out=h_grouped[:].bitcast(F32).rearrange("p (a r u) -> p a r u", a=C // P, u=2),
-                in_=turned(e).rearrange("p a u r -> p a r u"),
+                in_=turn[e][:].rearrange("p a u r -> p a r u"),
             )
+            h_codes[e] = held([P, C], U32, f"h_codes{e}", codes_home)
+            h_scales[e] = held([P, C], U8, f"h_scales{e}")
             nc.vector.quantize_mx(out=h_codes[e][:].bitcast(FP8X4), scales=h_scales[e][:], in_=h_grouped[:])
 
-        y_sb = {}
-
-        def second_layer(e, b):
-            bank = banks[y_bank[e, b]]
-            for c in range(2):
-                cols = slice((2 * b + c) * P, (2 * b + c + 1) * P)
+        def second_layer(e, blocks, bank_tag, spent=None):
+            bank = psum.tile([P, len(blocks), C], F32, name=f"y{e}_{blocks[0]}", tag=bank_tag)
+            for c, n in enumerate(blocks):
+                cols = slice(n * P, (n + 1) * P)
                 nc.tensor.matmul_mx(
-                    out=bank[:, c * C : (c + 1) * C],
+                    out=bank[:, c, :],
                     lhsT=codes[f"w2_{e}"][:, cols].bitcast(FP8X4),
                     lhsT_scale=scales[f"w2_{e}"][:, cols],
                     rhs=h_codes[e][:].bitcast(FP8X4),
@@ -240,117 +193,62 @@ def tile_moe_duo_none_kernel(
                     start=True,
                     stop=True,
                 )
-            if (e, b) in y_home:
-                name, half, row = y_home[e, b]
-                y_pair = raw[name, half][:, row : row + 2, :]
+            if spent is None:
+                rows = held([P, len(blocks), C], F32, f"y_sb{e}_{blocks[0]}")[:]
             else:
-                y_pair = held([P, 2, C], F32, f"y_pair{e}_{b}")[:]
-            nc.scalar.copy(out=y_pair, in_=bank[:].rearrange("p (c j) -> p c j", c=2))
-            y_sb[e, b] = y_pair
+                rows = raw[spent][:, blocks[0] : blocks[0] + len(blocks), 0:C]
+            nc.scalar.copy(out=rows, in_=bank[:])
+            for c, n in enumerate(blocks):
+                y_sb[e, n] = rows[:, c, :]
 
-        scattered = {}
+        def scatter(e, blocks, home=None):
+            for n in blocks:
+                if e == 0:
+                    windows[n] = held([P, T], F32, f"window{n}", home if n == blocks[0] else None)
+                nc.vector.tensor_tensor(
+                    windows[n][:].indirect(own_list[:, e * C // 16 : (e + 1) * C // 16]),
+                    y_sb[e, n],
+                    gate_sb[:, e * C : (e + 1) * C],
+                    MULT,
+                )
+                if e == E - 1:
+                    nc.sync.dma_start(out=out[n * P : (n + 1) * P, :], in_=windows[n][:])
 
-        def scatter(e, n):
-            nc.vector.tensor_tensor(
-                windows[n][:].indirect(own_list[:, e * C // 16 : (e + 1) * C // 16]),
-                y_sb[e, n // 2][:, n % 2, :],
-                gate_sb[:, e * C : (e + 1) * C],
-                MULT,
-            )
-            scattered[n] = scattered.get(n, 0) + 1
-            if scattered[n] == E:
-                nc.sync.dma_start(out=out[n * P : (n + 1) * P, :], in_=windows[n][:])
-
-        cast("w1_0_1", 1)
-        cast("w1_0_0", 0)
-        cast("w1_1_1", 1)
-        cast_vector("w2_1", 0)
-        gather(mate_words[1], mate_place, x_win[1][:].bitcast(U32), mate_list, 0, 1)
-        gather(mate_scales[0], every_place, both_win[:], mate_list, 2, 1)
-        gather(mate_words[0], mate_place, x_win[0][:].bitcast(U32), mate_list, 0, 1)
-        gather(mate_scales[0], every_place, both_win[:], mate_list, 0, 2)
-        gather(own_words[0], own_place, x_win[0][:].bitcast(U32), own_list, 0, 2)
-        cast_vector("w1_0_0", 1)
-        cast("w1_0_1", 0)
-        cast_vector("w1_2_0", 0)
-        move_mate_scales()
-        quantize("w1_0_0", 0, H)
-        quantize("w1_0_1", 0, H)
-        mate_pass(0, 0, 0)
-        mate_pass(0, 1, 0)
-        mate_pass(0, 0, 1)
-        gather(mate_words[0], mate_place, x_win[0][:].bitcast(U32), mate_list, 1, 1)
-        mate_pass(0, 1, 1)
-        gather(mate_words[1], mate_place, x_win[1][:].bitcast(U32), mate_list, 1, 1)
-        cast("w1_1_1", 0)
-        mate_pass(1, 1, 0)
-        gather(own_words[1], own_place, x_win[1][:].bitcast(U32), own_list, 0, 2)
-        gather(own_scales, own_place, both_win[:], own_list, 0, 2)
-        quantize("w1_1_1", 0, H)
-        cast("w1_1_0", 0)
-        own_pass(0, 1, 1)
-        own_pass(1, 0, 1)
-        mate_pass(1, 0, 0)
-        own_pass(0, 0, 1)
-        cast("w1_2_1", 1)
-        mate_pass(1, 0, 1)
-        cast_vector("w1_2_0", 1)
-        cast("w2_0", 0)
-        cast_vector("w2_1", 1)
-        own_pass(0, 1, 0)
-        cast("w1_2_1", 0)
-        turn_h(0, 1)
-        own_pass(0, 0, 0)
-        gather(own_words[1], own_place, x_win[1][:].bitcast(U32), own_list, 2, 1)
-        cast("w2_0", 1)
-        turn_h(0, 0)
-        cast("w1_1_0", 1)
-        own_pass(1, 1, 1)
-        mate_pass(1, 1, 1)
-        quantize("w1_1_0", 0, H)
-        gather(mate_words[0], mate_place, x_win[0][:].bitcast(U32), mate_list, 2, 1)
-        quantize("w1_2_1", 0, H)
-        own_pass(1, 0, 0)
-        quantize("w2_0", 0, H)
-        own_pass(1, 1, 0)
-        quantize_h(0)
-        quantize("w1_2_0", 0, H)
-        second_layer(0, 1)
-        gather(mate_words[1], mate_place, x_win[1][:].bitcast(U32), mate_list, 2, 1)
-        second_layer(0, 0)
-        cast("w2_2", 1)
-        quantize("w2_1", 0, H)
-        scatter(0, 1)
-        gather(own_scales, own_place, both_win[:], own_list, 2, 1)
-        gather(own_words[0], own_place, x_win[0][:].bitcast(U32), own_list, 2, 1)
-        scatter(0, 0)
-        mate_pass(2, 1, 1)
-        turn_h(1, 0)
-        cast("w2_2", 0)
-        own_pass(2, 0, 1)
-        own_pass(2, 1, 0)
-        mate_pass(2, 0, 1)
-        quantize("w2_2", 0, H)
-        mate_pass(2, 0, 0)
-        turn_h(1, 1)
-        own_pass(2, 1, 1)
-        quantize_h(1)
-        second_layer(1, 0)
-        scatter(1, 0)
-        mate_pass(2, 1, 0)
-        turn_h(2, 1)
-        own_pass(2, 0, 0)
-        turn_h(2, 0)
-        quantize_h(2)
-        second_layer(1, 1)
-        scatter(0, 3)
-        scatter(1, 3)
-        second_layer(2, 0)
-        scatter(0, 2)
-        second_layer(2, 1)
-        scatter(1, 1)
-        scatter(1, 2)
-        scatter(2, 0)
-        scatter(2, 1)
-        scatter(2, 2)
-        scatter(2, 3)
+        for s in range(PASSES):
+            gather_words("mate", 0, 1, s)
+            gather_words("own", 0, 1, s)
+            quantize_matrix(f"w1_0_{s}")
+        first_layer(0, [("own", 0), ("mate", 0), ("mate", 1)])
+        turn_h(0, None)
+        quantize_matrix("w2_0", vector_from=0)
+        gather_words("mate", 1, 2, 0)
+        gather_words("own", 1, 2, 0, "grouped_w1_0_0")
+        gather_words("mate", 1, 2, 1, "grouped_w1_0_1")
+        gather_words("own", 1, 2, 1, "raw_w1_0_1")
+        quantize_h(0, None)
+        quantize_matrix("w1_1_0")
+        second_layer(0, [0, 1], "y0")
+        second_layer(0, [2, 3], "y1")
+        scatter(0, [0, 1])
+        quantize_matrix("w1_1_1")
+        scatter(0, [2], "grouped_w1_1_1")
+        first_layer(1, [("own", 0), ("mate", 0), ("mate", 1)])
+        turn_h(1, None)
+        quantize_matrix("w2_1", vector_from=H)
+        scatter(0, [3], "grouped_w2_1")
+        quantize_h(1, None)
+        quantize_matrix("w1_2_0", codes_home="h_grouped1")
+        second_layer(1, [0, 1], "y0")
+        quantize_matrix("w1_2_1", vector_from=H // 2)
+        first_layer(2, [("own", 0), ("mate", 0), ("mate", 1)])
+        turn_h(2, None)
+        quantize_matrix("w2_2", "grouped_w1_2_1")
+        scatter(1, [0, 1])
+        second_layer(1, [2], "acc0")
+        quantize_h(2, None)
+        scatter(1, [2])
+        second_layer(1, [3], "turn0")
+        second_layer(2, [0, 1], "y1")
+        second_layer(2, [2, 3], "y0")
+        scatter(1, [3])
+        scatter(2, [0, 1, 2, 3])

@@ -1,7 +1,6 @@
 from contextlib import ExitStack
 
 import concourse.mybir as mybir
-from concourse.masks import make_identity
 
 K, T, E, C, H, N = 1024, 768, 3, 256, 512, 512
 FLOPS = 2 * E * C * (2 * K * H + H * N)
@@ -15,13 +14,15 @@ U8 = mybir.dt.uint8
 FP8X4 = mybir.dt.float8_e4m3fn_x4
 FP4X4 = mybir.dt.float4_e2m1fn_x4
 MULT = mybir.AluOpType.mult
+COPY = mybir.ActivationFunctionType.Copy
 
 P = 128
 PACK = 4
 K_PASS = P * PACK
 PASSES = K // K_PASS
 QUADS = 4
-LINE = 2
+RUN = 4
+SCALE_COLS = 1024
 
 
 def tile_moe_duo_none_kernel(
@@ -37,24 +38,22 @@ def tile_moe_duo_none_kernel(
 
         own_list = keep.tile([P, T // 16], U16, name="own_list")
         mate_list = keep.tile([P, T // 16], U16, name="mate_list")
-        x_win = [held([P, T], I32, f"x_win{s}") for s in range(PASSES)]
-        scale_win = held([P, T], U8, "scale_win")
+        x_win = held([P, PASSES, T], I32, "x_win")
+        scale_win = held([P, SCALE_COLS], U8, "scale_win")
         own_scales = held([P, T], U8, "own_scales")
         mate_scales = [held([P, T], U8, f"mate_scales{s}") for s in range(PASSES)]
-        wp_plane = held([P, E * PASSES, H], U8, "wp_plane")
+        plane_first = held([P, PASSES, H], U8, "plane_first")
+        plane_later = held([P, (E - 1) * PASSES, H], U8, "plane_later")
         wp_sb = [held([P, PASSES, 2 * H], U8, f"wp_sb{e}") for e in range(E)]
-        gate_sb = held([P, T], F32, "gate_sb")
-        ident = held([P, P], F32, "ident")
+        wp_dealt = [held([P, PASSES, 2 * H], U8, f"wp_dealt{e}") for e in range(E)]
+        gate_sb = [held([P, C], F32, f"gate_sb{e}") for e in range(E)]
 
         nc.vector.memset(scale_win[:].bitcast(I32), 0)
-        nc.vector.memset(wp_plane[:].rearrange("p a i -> p (a i)").bitcast(I32), 0)
+        nc.vector.memset(plane_first[:].rearrange("p a i -> p (a i)").bitcast(I32), 0)
+        nc.gpsimd.memset(plane_later[:].rearrange("p a i -> p (a i)").bitcast(I32), 0)
         nc.vector.memset(mate_scales[1][:].bitcast(I32), 0)
-        make_identity(nc, ident[:])
 
         raw = {}
-
-        def load_x(s):
-            nc.sync.dma_start(out=x_win[s][:], in_=x_words[s].rearrange("p t d -> p (t d)").bitcast(I32))
 
         def load_matrix(name, rows):
             raw[name] = held([P, PACK, H], F32, f"raw_{name}")
@@ -63,192 +62,250 @@ def tile_moe_duo_none_kernel(
         def load_w1(e, s):
             load_matrix(f"w1_{e}_{s}", w1[e, s * K_PASS : (s + 1) * K_PASS, :])
 
+        def load_w2(e):
+            raw[f"w2_{e}"] = held([P, PACK, N], F32, f"raw_w2_{e}")
+            rows = w2[e].rearrange("(m r j) n -> r m j n", r=PACK, j=RUN)
+            for r in range(PACK):
+                nc.sync.dma_start(out=raw[f"w2_{e}"][:, r, :], in_=rows[r])
+
         def load_wp(e):
             nc.sync.dma_start(
                 out=wp_sb[e][:].bitcast(I32), in_=wp_words[e].rearrange("s p b -> p s b").bitcast(I32)
             )
 
-        nc.sync.dma_start(mate_list[:], offs2)
-        nc.sync.dma_start(own_list[:], offs)
-        for q in range(QUADS):
-            nc.sync.dma_start(
-                out=scale_win[32 * q : 32 * q + 8, :].bitcast(I32),
-                in_=x_scales[:, 4 * q : 4 * q + 4, :].bitcast(I32),
-            )
-        load_x(0)
-        load_w1(0, 0)
-        load_w1(0, 1)
-        load_wp(0)
-        for q in range(QUADS):
-            nc.sync.dma_start(
-                out=wp_plane[32 * q : 32 * q + 4, :, :].bitcast(I32),
-                in_=wp_scales[:, :, 4 * q : 4 * q + 4, :].rearrange("e s r i -> r (e s) i").bitcast(I32),
-            )
+        def load_gate(e):
+            nc.sync.dma_start(out=gate_sb[e][:], in_=gate[:, e * C : (e + 1) * C])
 
         def gather(dst, window, offsets, first, count):
             nc.vector.tensor_copy(out=dst, in_=window.indirect(offsets[:, first // 16 : (first + count) // 16]))
 
-        for first, count in ((0, 2 * C), (2 * C, C)):
-            gather(mate_scales[0][:, first : first + count], scale_win[:], mate_list, first, count)
+        nc.sync.dma_start(mate_list[:], offs2)
+        nc.sync.dma_start(own_list[:], offs)
+        for q in range(QUADS):
+            nc.sync.dma_start(
+                out=scale_win[32 * q : 32 * q + 8, 0:T].bitcast(I32),
+                in_=x_scales[:, 4 * q : 4 * q + 4, :].bitcast(I32),
+            )
+        load_wp(0)
+        nc.sync.dma_start(out=x_win[:], in_=x_words.rearrange("s p t d -> p s (t d)").bitcast(I32))
+        for r in range(4):
+            nc.sync.dma_start(
+                out=plane_first[r:P:32, :, :].bitcast(I32),
+                in_=wp_scales[0, :, r:16:4, :].rearrange("s q i -> q s i").bitcast(I32),
+            )
+            nc.gpsimd.dma_start(
+                out=plane_later[r:P:32, :, :].bitcast(I32),
+                in_=wp_scales[1:, :, r:16:4, :].rearrange("e s q i -> q (e s) i").bitcast(I32),
+            )
+        load_w1(0, 0)
+        gather(mate_scales[0][:], scale_win[:], mate_list, 0, T)
         nc.sync.dma_start(out=mate_scales[1][0:100, :].bitcast(I32), in_=mate_scales[0][4:104, :].bitcast(I32))
-        for first, count in ((0, 2 * C), (2 * C, C)):
-            gather(own_scales[:, first : first + count], scale_win[:], own_list, first, count)
+        gather(own_scales[:], scale_win[:], own_list, 0, T)
+        load_w1(0, 1)
+        load_w2(0)
+        load_w1(1, 0)
+        load_wp(1)
+        load_gate(0)
+        load_w1(1, 1)
+        load_w2(1)
+        load_wp(2)
+        load_w1(2, 0)
+        load_gate(1)
+        load_w1(2, 1)
+        load_w2(2)
+        load_gate(2)
 
-        load_x(1)
-        load_matrix("w2_0", w2[0])
-        for e in range(1, E):
-            load_w1(e, 0)
-            load_w1(e, 1)
-            if e == 1:
-                nc.sync.dma_start(out=gate_sb[:], in_=gate)
-            load_wp(e)
-            load_matrix(f"w2_{e}", w2[e])
+        grouped, codes, scales = {}, {}, {}
+        windows, wp_scale = {}, {}
+        words, acc, h_grouped, h_codes, h_scales, bank, y_sb = {}, {}, {}, {}, {}, {}, {}
 
-        codes, scales = {}, {}
+        def move(engine, dst, src):
+            if engine == "scalar":
+                nc.scalar.copy(out=dst, in_=src)
+            else:
+                nc.vector.tensor_copy(out=dst, in_=src)
 
-        def quantize_matrix(name, home=None, vector_from=H, codes_home=None, pieces=1):
-            grouped = held([P, H, PACK], BF16, f"grouped_{name}", home)
-            dst = grouped[:].rearrange("p (c i) t -> p c t i", i=LINE)
-            src = raw[name][:].rearrange("p t (c i) -> p c t i", i=LINE)
-            width = vector_from // LINE // pieces
-            for piece in range(pieces if vector_from > 0 else 0):
-                cols = slice(piece * width, (piece + 1) * width)
-                nc.scalar.copy(out=dst[:, cols], in_=src[:, cols])
-            if vector_from < H:
-                nc.vector.tensor_copy(out=dst[:, vector_from // LINE :], in_=src[:, vector_from // LINE :])
-            codes[name] = held([P, H], U32, f"codes_{name}", codes_home)
+        def cast(name, engine):
+            grouped[name] = held([P, H, PACK], BF16, f"grouped_{name}")
+            if name.startswith("w1"):
+                dst = grouped[name][:].rearrange("p (r m j) t -> p m r t j", r=PACK, j=RUN)
+                src = raw[name][:].rearrange("p t (m r j) -> p m r t j", r=PACK, j=RUN)
+            else:
+                dst = grouped[name][:].rearrange("p (c j) t -> p c t j", j=RUN)
+                src = raw[name][:].rearrange("p t (c j) -> p c t j", j=RUN)
+            move(engine, dst, src)
+
+        def deal_wp(e):
+            nc.scalar.copy(
+                out=wp_dealt[e][:].bitcast(U32).rearrange("p s (r m w) -> p s m r w", r=PACK, w=RUN // 2),
+                in_=wp_sb[e][:].bitcast(U32).rearrange("p s (m r w) -> p s m r w", r=PACK, w=RUN // 2),
+            )
+
+        def deal_plane(plane, first, count, engine, dtype, home=None):
+            dealt = held([P, count * PASSES, H], U8, f"plane_dealt{first}", home)
+            move(
+                engine,
+                dealt[:].bitcast(dtype).rearrange("p a (r m) -> p a m r", r=PACK),
+                plane[:].bitcast(dtype).rearrange("p a (m r) -> p a m r", r=PACK),
+            )
+            for e in range(count):
+                for s in range(PASSES):
+                    wp_scale[first + e, s] = dealt[:, e * PASSES + s, :]
+
+        def quantize(name):
+            codes[name] = held([P, H], U32, f"codes_{name}")
             scales[name] = held([P, H], U8, f"scales_{name}")
             nc.vector.quantize_mx(
                 out=codes[name][:].bitcast(FP8X4),
                 scales=scales[name][:],
-                in_=grouped[:].rearrange("p c t -> p (c t)"),
+                in_=grouped[name][:].rearrange("p c t -> p (c t)"),
             )
 
-        windows = {}
-        words, acc, turn, h_codes, h_scales, y_sb = {}, {}, {}, {}, {}, {}
+        def gather_words(wanted, home=None):
+            kind, e, s = wanted[0]
+            tile = held([P, len(wanted) * C], U32, f"words_{kind}{e}_{s}", home)
+            for place, (kind, e, s) in enumerate(wanted):
+                words[kind, e, s] = tile[:, place * C : (place + 1) * C]
+                offsets = mate_list if kind == "mate" else own_list
+                gather(words[kind, e, s], x_win[:, s, :].bitcast(U32), offsets, e * C, C)
 
-        def gather_words(kind, first, count, s, home=None):
-            tile = held([P, count * C], U32, f"words_{kind}{first}_{s}", home)
-            gather(tile[:], x_win[s][:].bitcast(U32), mate_list if kind == "mate" else own_list, first * C, count * C)
-            for e in range(count):
-                words[kind, first + e, s] = tile[:, e * C : (e + 1) * C]
-
-        def first_layer(e, order):
+        def first_layer(e, steps):
             for a in range(C // P):
-                acc[e, a] = psum.tile([P, H], F32, name=f"acc{e}_{a}", tag=f"acc{a}")
-            for step, (kind, s) in enumerate(order + [("own", 1)]):
+                acc[e, a] = psum.tile([P, PACK, P], F32, name=f"acc{e}_{a}", tag=f"acc{e % 2}_{a}")
+            for step, (kind, s) in enumerate(steps):
+                last = step == len(steps) - 1
                 for a in range(C // P):
-                    here = slice(a * P, (a + 1) * P)
-                    slots = slice(e * C + a * P, e * C + (a + 1) * P)
-                    if kind == "mate":
-                        lhsT, lhsT_scale = words[kind, e, s][:, here], mate_scales[s][:, slots]
-                        rhs, rhs_scale = wp_sb[e][:, s, :].bitcast(FP4X4), wp_plane[:, e * PASSES + s, :]
-                    else:
-                        lhsT, lhsT_scale = words[kind, e, s][:, here], own_scales[4 * s :, slots]
-                        rhs, rhs_scale = codes[f"w1_{e}_{s}"][:].bitcast(FP8X4), scales[f"w1_{e}_{s}"][:]
+                    for r in range(PACK):
+                        here = slice(a * P, (a + 1) * P)
+                        slots = slice(e * C + a * P, e * C + (a + 1) * P)
+                        cols = slice(r * P, (r + 1) * P)
+                        if kind == "mate":
+                            lhsT = wp_dealt[e][:, s, 2 * r * P : 2 * (r + 1) * P].bitcast(FP4X4)
+                            lhsT_scale = wp_scale[e, s][:, cols]
+                            rhs_scale = mate_scales[s][:, slots]
+                        else:
+                            lhsT = codes[f"w1_{e}_{s}"][:, cols].bitcast(FP8X4)
+                            lhsT_scale = scales[f"w1_{e}_{s}"][:, cols]
+                            rhs_scale = own_scales[4 * s :, slots]
+                        nc.tensor.matmul_mx(
+                            out=acc[e, a][:, r, :],
+                            lhsT=lhsT,
+                            lhsT_scale=lhsT_scale,
+                            rhs=words[kind, e, s][:, here].bitcast(FP8X4),
+                            rhs_scale=rhs_scale,
+                            start=(step == 0 and r == 0),
+                            stop=(last and r == PACK - 1),
+                        )
+
+        def round_h(e, engine):
+            h_grouped[e] = held([P, C // P, P, PACK], BF16, f"h_grouped{e}")
+            for a in range(C // P):
+                move(engine, h_grouped[e][:, a], acc[e, a][:].rearrange("p r c -> p c r"))
+
+        def quantize_h(e):
+            h_codes[e] = held([P, C], U32, f"h_codes{e}")
+            h_scales[e] = held([P, C], U8, f"h_scales{e}")
+            nc.vector.quantize_mx(
+                out=h_codes[e][:].bitcast(FP8X4),
+                scales=h_scales[e][:],
+                in_=h_grouped[e][:].rearrange("p a c r -> p (a c r)"),
+            )
+
+        def second_layer(e, groups):
+            for place, blocks in enumerate(groups):
+                bank[e, blocks] = psum.tile([P, len(blocks), C], F32, name=f"y{e}_{place}", tag=f"y{place}")
+                for c, n in enumerate(blocks):
+                    cols = slice(n * P, (n + 1) * P)
                     nc.tensor.matmul_mx(
-                        out=acc[e, a][:],
-                        lhsT=lhsT.bitcast(FP8X4),
-                        lhsT_scale=lhsT_scale,
-                        rhs=rhs,
-                        rhs_scale=rhs_scale,
-                        start=(step == 0),
-                        stop=(kind == "own" and s == PASSES - 1),
+                        out=bank[e, blocks][:, c, :],
+                        lhsT=codes[f"w2_{e}"][:, cols].bitcast(FP8X4),
+                        lhsT_scale=scales[f"w2_{e}"][:, cols],
+                        rhs=h_codes[e][:].bitcast(FP8X4),
+                        rhs_scale=h_scales[e][:],
+                        start=True,
+                        stop=True,
                     )
 
-        def turn_h(e, home):
-            turn[e] = psum.tile([P, C // P, 2, P], F32, name=f"turn{e}", tag=f"turn{e % 2}")
-            for a in range(C // P):
-                if home is None:
-                    pairs = held([P, H // 2], F32, f"h_rows{e}_{a}")[:]
-                else:
-                    pairs = raw[home][:, a, 0 : H // 2]
-                nc.scalar.copy(
-                    out=pairs.bitcast(BF16).rearrange("s (u p v) -> s u p v", u=2, v=2),
-                    in_=acc[e, a][:].rearrange("s (p u v) -> s u p v", u=2, v=2),
-                )
-                for u in range(2):
-                    nc.tensor.transpose(turn[e][:, a, u, :], pairs[:, u * P : (u + 1) * P], ident[:])
-
-        def quantize_h(e, home, codes_home=None):
-            h_grouped = held([P, C * PACK], BF16, f"h_grouped{e}", home)
-            nc.scalar.copy(
-                out=h_grouped[:].bitcast(F32).rearrange("p (a r u) -> p a r u", a=C // P, u=2),
-                in_=turn[e][:].rearrange("p a u r -> p a r u"),
-            )
-            h_codes[e] = held([P, C], U32, f"h_codes{e}", codes_home)
-            h_scales[e] = held([P, C], U8, f"h_scales{e}")
-            nc.vector.quantize_mx(out=h_codes[e][:].bitcast(FP8X4), scales=h_scales[e][:], in_=h_grouped[:])
-
-        def second_layer(e, blocks, bank_tag, spent=None):
-            bank = psum.tile([P, len(blocks), C], F32, name=f"y{e}_{blocks[0]}", tag=bank_tag)
-            for c, n in enumerate(blocks):
-                cols = slice(n * P, (n + 1) * P)
-                nc.tensor.matmul_mx(
-                    out=bank[:, c, :],
-                    lhsT=codes[f"w2_{e}"][:, cols].bitcast(FP8X4),
-                    lhsT_scale=scales[f"w2_{e}"][:, cols],
-                    rhs=h_codes[e][:].bitcast(FP8X4),
-                    rhs_scale=h_scales[e][:],
-                    start=True,
-                    stop=True,
-                )
-            if spent is None:
-                rows = held([P, len(blocks), C], F32, f"y_sb{e}_{blocks[0]}")[:]
+        def leave(e, blocks, engine, home=None):
+            rows = held([P, len(blocks), C], F32, f"y_sb{e}_{blocks[0]}", home)
+            if engine == "scalar":
+                nc.scalar.copy(out=rows[:], in_=bank[e, blocks][:])
             else:
-                rows = raw[spent][:, blocks[0] : blocks[0] + len(blocks), 0:C]
-            nc.scalar.copy(out=rows, in_=bank[:])
+                weights = gate_sb[e][:].unsqueeze(1).to_broadcast([P, len(blocks), C])
+                nc.vector.tensor_tensor(rows[:], bank[e, blocks][:], weights, MULT)
             for c, n in enumerate(blocks):
                 y_sb[e, n] = rows[:, c, :]
 
-        def scatter(e, blocks, home=None):
-            for n in blocks:
-                if e == 0:
-                    windows[n] = held([P, T], F32, f"window{n}", home if n == blocks[0] else None)
-                nc.vector.tensor_tensor(
-                    windows[n][:].indirect(own_list[:, e * C // 16 : (e + 1) * C // 16]),
-                    y_sb[e, n],
-                    gate_sb[:, e * C : (e + 1) * C],
-                    MULT,
-                )
-                if e == E - 1:
-                    nc.sync.dma_start(out=out[n * P : (n + 1) * P, :], in_=windows[n][:])
+        def scatter(e, n, engine, home=None):
+            if e == 0:
+                windows[n] = held([P, T], F32, f"window{n}", home)
+            target = windows[n][:].indirect(own_list[:, e * C // 16 : (e + 1) * C // 16])
+            if engine == "scalar":
+                nc.scalar.activation(target, y_sb[e, n], COPY)
+            else:
+                nc.vector.tensor_tensor(target, y_sb[e, n], gate_sb[e][:], MULT)
+            if e == E - 1:
+                nc.sync.dma_start(out=out[n * P : (n + 1) * P, :], in_=windows[n][:])
 
-        for s in range(PASSES):
-            gather_words("mate", 0, 1, s)
-            gather_words("own", 0, 1, s)
-            quantize_matrix(f"w1_0_{s}")
-        first_layer(0, [("own", 0), ("mate", 0), ("mate", 1)])
-        turn_h(0, None)
-        quantize_matrix("w2_0", vector_from=0)
-        gather_words("mate", 1, 2, 0)
-        gather_words("own", 1, 2, 0, "grouped_w1_0_0")
-        gather_words("mate", 1, 2, 1, "grouped_w1_0_1")
-        gather_words("own", 1, 2, 1, "raw_w1_0_1")
-        quantize_h(0, None)
-        quantize_matrix("w1_1_0")
-        second_layer(0, [0, 1], "y0")
-        second_layer(0, [2, 3], "y1")
-        scatter(0, [0, 1])
-        quantize_matrix("w1_1_1")
-        scatter(0, [2], "grouped_w1_1_1")
-        first_layer(1, [("own", 0), ("mate", 0), ("mate", 1)])
-        turn_h(1, None)
-        quantize_matrix("w2_1", vector_from=H)
-        scatter(0, [3], "grouped_w2_1")
-        quantize_h(1, None)
-        quantize_matrix("w1_2_0", codes_home="h_grouped1")
-        second_layer(1, [0, 1], "y0")
-        quantize_matrix("w1_2_1", vector_from=H // 2)
-        first_layer(2, [("own", 0), ("mate", 0), ("mate", 1)])
-        turn_h(2, None)
-        quantize_matrix("w2_2", "grouped_w1_2_1")
-        scatter(1, [0, 1])
-        second_layer(1, [2], "acc0")
-        quantize_h(2, None)
-        scatter(1, [2])
-        second_layer(1, [3], "turn0")
-        second_layer(2, [0, 1], "y1")
-        second_layer(2, [2, 3], "y0")
-        scatter(1, [3])
-        scatter(2, [0, 1, 2, 3])
+        deal_wp(0)
+        deal_plane(plane_first, 0, 1, "scalar", U32)
+        gather_words([("mate", 0, 0), ("mate", 0, 1), ("own", 0, 0), ("own", 0, 1)])
+        gather_words([("mate", 1, 0), ("mate", 1, 1)])
+        cast("w1_0_0", "scalar")
+        quantize("w1_0_0")
+        cast("w1_0_1", "scalar")
+        quantize("w1_0_1")
+        gather_words([("own", 1, 0), ("own", 1, 1), ("mate", 2, 0)], "grouped_w1_0_0")
+        first_layer(0, [("mate", 0), ("mate", 1), ("own", 0), ("own", 1)])
+        round_h(0, "vector")
+        gather_words([("mate", 2, 1)], "grouped_w1_0_1")
+        cast("w2_0", "scalar")
+        quantize("w2_0")
+        quantize_h(0)
+        deal_plane(plane_later, 1, E - 1, "vector", I32, "grouped_w2_0")
+        cast("w1_1_0", "scalar")
+        deal_wp(1)
+        second_layer(0, [(0, 1), (2, 3)])
+        leave(0, (0, 1), "vector", "raw_w1_1_0")
+        gather_words([("own", 2, 0)], "h_grouped0")
+        scatter(0, 0, "scalar")
+        scatter(0, 1, "scalar")
+
+        quantize("w1_1_0")
+        cast("w1_1_1", "vector")
+        quantize("w1_1_1")
+        first_layer(1, [("mate", 0), ("mate", 1), ("own", 0), ("own", 1)])
+        round_h(1, "scalar")
+        leave(0, (2, 3), "vector", "codes_w1_1_1")
+        cast("w2_1", "vector")
+        quantize("w2_1")
+        deal_wp(2)
+        scatter(0, 2, "scalar")
+        scatter(0, 3, "scalar")
+        quantize_h(1)
+        gather_words([("own", 2, 1)], "grouped_w2_1")
+        second_layer(1, [(0, 1), (2,), (3,)])
+        cast("w1_2_0", "vector")
+        leave(1, (0, 1), "vector")
+        scatter(1, 0, "scalar")
+        scatter(1, 1, "scalar")
+
+        quantize("w1_2_0")
+        cast("w1_2_1", "vector")
+        quantize("w1_2_1")
+        first_layer(2, [("mate", 0), ("mate", 1), ("own", 0), ("own", 1)])
+        round_h(2, "scalar")
+        leave(1, (3,), "scalar", "codes_w1_2_1")
+        leave(1, (2,), "vector", "scales_w1_2_1")
+        cast("w2_2", "vector")
+        quantize("w2_2")
+        scatter(1, 2, "scalar")
+        quantize_h(2)
+        scatter(1, 3, "vector")
+        second_layer(2, [(0, 1), (2, 3)])
+        leave(2, (0, 1), "vector")
+        leave(2, (2, 3), "scalar")
+        scatter(2, 0, "scalar")
+        scatter(2, 1, "scalar")
+        scatter(2, 2, "vector")
+        scatter(2, 3, "vector")

from contextlib import ExitStack

import concourse.mybir as mybir

K, T, E, C, H, N = 1024, 768, 3, 256, 512, 512
FLOPS = 2 * E * C * (2 * K * H + H * N)

F32 = mybir.dt.float32
BF16 = mybir.dt.bfloat16
I32 = mybir.dt.int32
U32 = mybir.dt.uint32
U16 = mybir.dt.uint16
U8 = mybir.dt.uint8
FP8X4 = mybir.dt.float8_e4m3fn_x4
FP4X4 = mybir.dt.float4_e2m1fn_x4
MULT = mybir.AluOpType.mult
COPY = mybir.ActivationFunctionType.Copy

P = 128
PACK = 4
K_PASS = P * PACK
PASSES = K // K_PASS
QUADS = 4
RUN = 4
SCALE_COLS = 1024


def tile_moe_duo_none_kernel(
    tc, x_words, x_scales, w1, wp_words, wp_scales, w2, gate, offs, offs2, out
):
    nc = tc.nc
    with ExitStack() as ctx:
        keep = ctx.enter_context(tc.tile_pool(name="keep", bufs=1))
        psum = ctx.enter_context(tc.psum_pool(name="psum", bufs=1))

        def held(shape, dtype, name, tag=None):
            return keep.tile(shape, dtype, name=name, tag=tag or name, align_bytes=64)

        own_list = keep.tile([P, T // 16], U16, name="own_list")
        mate_list = keep.tile([P, T // 16], U16, name="mate_list")
        x_win = held([P, PASSES, T], I32, "x_win")
        scale_win = held([P, SCALE_COLS], U8, "scale_win")
        own_scales = held([P, T], U8, "own_scales")
        mate_scales = [held([P, T], U8, f"mate_scales{s}") for s in range(PASSES)]
        plane_first = held([P, PASSES, H], U8, "plane_first")
        plane_later = held([P, (E - 1) * PASSES, H], U8, "plane_later")
        wp_sb = [held([P, PASSES, 2 * H], U8, f"wp_sb{e}") for e in range(E)]
        wp_dealt = [held([P, PASSES, 2 * H], U8, f"wp_dealt{e}") for e in range(E)]
        gate_sb = [held([P, C], F32, f"gate_sb{e}") for e in range(E)]

        nc.vector.memset(scale_win[:].bitcast(I32), 0)
        nc.vector.memset(plane_first[:].rearrange("p a i -> p (a i)").bitcast(I32), 0)
        nc.gpsimd.memset(plane_later[:].rearrange("p a i -> p (a i)").bitcast(I32), 0)
        nc.vector.memset(mate_scales[1][:].bitcast(I32), 0)

        raw = {}

        def load_matrix(name, rows):
            raw[name] = held([P, PACK, H], F32, f"raw_{name}")
            nc.sync.dma_start(out=raw[name][:], in_=rows.rearrange("(p j) w -> p j w", j=PACK))

        def load_w1(e, s):
            load_matrix(f"w1_{e}_{s}", w1[e, s * K_PASS : (s + 1) * K_PASS, :])

        def load_w2(e):
            raw[f"w2_{e}"] = held([P, PACK, N], F32, f"raw_w2_{e}")
            rows = w2[e].rearrange("(m r j) n -> r m j n", r=PACK, j=RUN)
            for r in range(PACK):
                nc.sync.dma_start(out=raw[f"w2_{e}"][:, r, :], in_=rows[r])

        def load_wp(e):
            nc.sync.dma_start(
                out=wp_sb[e][:].bitcast(I32), in_=wp_words[e].rearrange("s p b -> p s b").bitcast(I32)
            )

        def load_gate(e):
            nc.sync.dma_start(out=gate_sb[e][:], in_=gate[:, e * C : (e + 1) * C])

        def gather(dst, window, offsets, first, count):
            nc.vector.tensor_copy(out=dst, in_=window.indirect(offsets[:, first // 16 : (first + count) // 16]))

        nc.sync.dma_start(mate_list[:], offs2)
        nc.sync.dma_start(own_list[:], offs)
        for q in range(QUADS):
            nc.sync.dma_start(
                out=scale_win[32 * q : 32 * q + 8, 0:T].bitcast(I32),
                in_=x_scales[:, 4 * q : 4 * q + 4, :].bitcast(I32),
            )
        load_wp(0)
        nc.sync.dma_start(out=x_win[:], in_=x_words.rearrange("s p t d -> p s (t d)").bitcast(I32))
        for r in range(4):
            nc.sync.dma_start(
                out=plane_first[r:P:32, :, :].bitcast(I32),
                in_=wp_scales[0, :, r:16:4, :].rearrange("s q i -> q s i").bitcast(I32),
            )
            nc.gpsimd.dma_start(
                out=plane_later[r:P:32, :, :].bitcast(I32),
                in_=wp_scales[1:, :, r:16:4, :].rearrange("e s q i -> q (e s) i").bitcast(I32),
            )
        load_w1(0, 0)
        gather(mate_scales[0][:], scale_win[:], mate_list, 0, T)
        nc.sync.dma_start(out=mate_scales[1][0:100, :].bitcast(I32), in_=mate_scales[0][4:104, :].bitcast(I32))
        gather(own_scales[:], scale_win[:], own_list, 0, T)
        load_w1(0, 1)
        load_w2(0)
        load_w1(1, 0)
        load_wp(1)
        load_gate(0)
        load_w1(1, 1)
        load_w2(1)
        load_wp(2)
        load_w1(2, 0)
        load_gate(1)
        load_w1(2, 1)
        load_w2(2)
        load_gate(2)

        grouped, codes, scales = {}, {}, {}
        windows, wp_scale = {}, {}
        words, acc, h_grouped, h_codes, h_scales, bank, y_sb = {}, {}, {}, {}, {}, {}, {}

        def move(engine, dst, src):
            if engine == "scalar":
                nc.scalar.copy(out=dst, in_=src)
            else:
                nc.vector.tensor_copy(out=dst, in_=src)

        def cast(name, engine):
            grouped[name] = held([P, H, PACK], BF16, f"grouped_{name}")
            if name.startswith("w1"):
                dst = grouped[name][:].rearrange("p (r m j) t -> p m r t j", r=PACK, j=RUN)
                src = raw[name][:].rearrange("p t (m r j) -> p m r t j", r=PACK, j=RUN)
            else:
                dst = grouped[name][:].rearrange("p (c j) t -> p c t j", j=RUN)
                src = raw[name][:].rearrange("p t (c j) -> p c t j", j=RUN)
            move(engine, dst, src)

        def deal_wp(e):
            nc.scalar.copy(
                out=wp_dealt[e][:].bitcast(U32).rearrange("p s (r m w) -> p s m r w", r=PACK, w=RUN // 2),
                in_=wp_sb[e][:].bitcast(U32).rearrange("p s (m r w) -> p s m r w", r=PACK, w=RUN // 2),
            )

        def deal_plane(plane, first, count, engine, dtype, home=None):
            dealt = held([P, count * PASSES, H], U8, f"plane_dealt{first}", home)
            move(
                engine,
                dealt[:].bitcast(dtype).rearrange("p a (r m) -> p a m r", r=PACK),
                plane[:].bitcast(dtype).rearrange("p a (m r) -> p a m r", r=PACK),
            )
            for e in range(count):
                for s in range(PASSES):
                    wp_scale[first + e, s] = dealt[:, e * PASSES + s, :]

        def quantize(name):
            codes[name] = held([P, H], U32, f"codes_{name}")
            scales[name] = held([P, H], U8, f"scales_{name}")
            nc.vector.quantize_mx(
                out=codes[name][:].bitcast(FP8X4),
                scales=scales[name][:],
                in_=grouped[name][:].rearrange("p c t -> p (c t)"),
            )

        def gather_words(wanted, home=None):
            kind, e, s = wanted[0]
            tile = held([P, len(wanted) * C], U32, f"words_{kind}{e}_{s}", home)
            for place, (kind, e, s) in enumerate(wanted):
                words[kind, e, s] = tile[:, place * C : (place + 1) * C]
                offsets = mate_list if kind == "mate" else own_list
                gather(words[kind, e, s], x_win[:, s, :].bitcast(U32), offsets, e * C, C)

        def first_layer(e, steps):
            for a in range(C // P):
                acc[e, a] = psum.tile([P, PACK, P], F32, name=f"acc{e}_{a}", tag=f"acc{e % 2}_{a}")
            for step, (kind, s) in enumerate(steps):
                last = step == len(steps) - 1
                for a in range(C // P):
                    for r in range(PACK):
                        here = slice(a * P, (a + 1) * P)
                        slots = slice(e * C + a * P, e * C + (a + 1) * P)
                        cols = slice(r * P, (r + 1) * P)
                        if kind == "mate":
                            lhsT = wp_dealt[e][:, s, 2 * r * P : 2 * (r + 1) * P].bitcast(FP4X4)
                            lhsT_scale = wp_scale[e, s][:, cols]
                            rhs_scale = mate_scales[s][:, slots]
                        else:
                            lhsT = codes[f"w1_{e}_{s}"][:, cols].bitcast(FP8X4)
                            lhsT_scale = scales[f"w1_{e}_{s}"][:, cols]
                            rhs_scale = own_scales[4 * s :, slots]
                        nc.tensor.matmul_mx(
                            out=acc[e, a][:, r, :],
                            lhsT=lhsT,
                            lhsT_scale=lhsT_scale,
                            rhs=words[kind, e, s][:, here].bitcast(FP8X4),
                            rhs_scale=rhs_scale,
                            start=(step == 0 and r == 0),
                            stop=(last and r == PACK - 1),
                        )

        def round_h(e, engine):
            h_grouped[e] = held([P, C // P, P, PACK], BF16, f"h_grouped{e}")
            for a in range(C // P):
                move(engine, h_grouped[e][:, a], acc[e, a][:].rearrange("p r c -> p c r"))

        def quantize_h(e):
            h_codes[e] = held([P, C], U32, f"h_codes{e}")
            h_scales[e] = held([P, C], U8, f"h_scales{e}")
            nc.vector.quantize_mx(
                out=h_codes[e][:].bitcast(FP8X4),
                scales=h_scales[e][:],
                in_=h_grouped[e][:].rearrange("p a c r -> p (a c r)"),
            )

        def second_layer(e, groups):
            for place, blocks in enumerate(groups):
                bank[e, blocks] = psum.tile([P, len(blocks), C], F32, name=f"y{e}_{place}", tag=f"y{place}")
                for c, n in enumerate(blocks):
                    cols = slice(n * P, (n + 1) * P)
                    nc.tensor.matmul_mx(
                        out=bank[e, blocks][:, c, :],
                        lhsT=codes[f"w2_{e}"][:, cols].bitcast(FP8X4),
                        lhsT_scale=scales[f"w2_{e}"][:, cols],
                        rhs=h_codes[e][:].bitcast(FP8X4),
                        rhs_scale=h_scales[e][:],
                        start=True,
                        stop=True,
                    )

        def leave(e, blocks, engine, home=None):
            rows = held([P, len(blocks), C], F32, f"y_sb{e}_{blocks[0]}", home)
            if engine == "scalar":
                nc.scalar.copy(out=rows[:], in_=bank[e, blocks][:])
            else:
                weights = gate_sb[e][:].unsqueeze(1).to_broadcast([P, len(blocks), C])
                nc.vector.tensor_tensor(rows[:], bank[e, blocks][:], weights, MULT)
            for c, n in enumerate(blocks):
                y_sb[e, n] = rows[:, c, :]

        def scatter(e, n, engine, home=None):
            if e == 0:
                windows[n] = held([P, T], F32, f"window{n}", home)
            target = windows[n][:].indirect(own_list[:, e * C // 16 : (e + 1) * C // 16])
            if engine == "scalar":
                nc.scalar.activation(target, y_sb[e, n], COPY)
            else:
                nc.vector.tensor_tensor(target, y_sb[e, n], gate_sb[e][:], MULT)
            if e == E - 1:
                nc.sync.dma_start(out=out[n * P : (n + 1) * P, :], in_=windows[n][:])

        deal_wp(0)
        deal_plane(plane_first, 0, 1, "scalar", U32)
        gather_words([("mate", 0, 0), ("mate", 0, 1), ("own", 0, 0), ("own", 0, 1)])
        gather_words([("mate", 1, 0), ("mate", 1, 1)])
        cast("w1_0_0", "scalar")
        quantize("w1_0_0")
        cast("w1_0_1", "scalar")
        quantize("w1_0_1")
        gather_words([("own", 1, 0), ("own", 1, 1), ("mate", 2, 0)], "grouped_w1_0_0")
        first_layer(0, [("mate", 0), ("mate", 1), ("own", 0), ("own", 1)])
        round_h(0, "vector")
        gather_words([("mate", 2, 1)], "grouped_w1_0_1")
        cast("w2_0", "scalar")
        quantize("w2_0")
        quantize_h(0)
        deal_plane(plane_later, 1, E - 1, "vector", I32, "grouped_w2_0")
        cast("w1_1_0", "scalar")
        deal_wp(1)
        second_layer(0, [(0, 1), (2, 3)])
        leave(0, (0, 1), "vector", "raw_w1_1_0")
        gather_words([("own", 2, 0)], "h_grouped0")
        scatter(0, 0, "scalar")
        scatter(0, 1, "scalar")

        quantize("w1_1_0")
        cast("w1_1_1", "vector")
        quantize("w1_1_1")
        first_layer(1, [("mate", 0), ("mate", 1), ("own", 0), ("own", 1)])
        round_h(1, "scalar")
        leave(0, (2, 3), "vector", "codes_w1_1_1")
        cast("w2_1", "vector")
        quantize("w2_1")
        deal_wp(2)
        scatter(0, 2, "scalar")
        scatter(0, 3, "scalar")
        quantize_h(1)
        gather_words([("own", 2, 1)], "grouped_w2_1")
        second_layer(1, [(0, 1), (2,), (3,)])
        cast("w1_2_0", "vector")
        leave(1, (0, 1), "vector")
        scatter(1, 0, "scalar")
        scatter(1, 1, "scalar")

        quantize("w1_2_0")
        cast("w1_2_1", "vector")
        quantize("w1_2_1")
        first_layer(2, [("mate", 0), ("mate", 1), ("own", 0), ("own", 1)])
        round_h(2, "scalar")
        leave(1, (3,), "scalar", "codes_w1_2_1")
        leave(1, (2,), "vector", "scales_w1_2_1")
        cast("w2_2", "vector")
        quantize("w2_2")
        scatter(1, 2, "scalar")
        quantize_h(2)
        scatter(1, 3, "vector")
        second_layer(2, [(0, 1), (2, 3)])
        leave(2, (0, 1), "vector")
        leave(2, (2, 3), "scalar")
        scatter(2, 0, "scalar")
        scatter(2, 1, "scalar")
        scatter(2, 2, "vector")
        scatter(2, 3, "vector")
